import numpy as np
import ml_dtypes


def mxq(x, axis, fmt="e4m3"):
    dtype, down = {"e4m3": (ml_dtypes.float8_e4m3fn, 7), "e5m2": (ml_dtypes.float8_e5m2, 14)}[fmt]
    v = np.moveaxis(np.asarray(x, np.float32).astype(ml_dtypes.bfloat16).astype(np.float64), axis, -1)
    blocks = v.reshape(v.shape[:-1] + (-1, 32))
    amax = np.abs(blocks).max(-1, keepdims=True)
    byte = np.maximum(np.where(amax > 0, np.frexp(amax)[1] - 1 + 127, 0) - down, 1)
    scale = np.exp2(byte - 127.0)
    codes = (blocks / scale).astype(np.float32).astype(dtype).astype(np.float64)
    return np.moveaxis((codes * scale).reshape(v.shape), -1, axis)


WIDE = False


def mx_kscale(k):
    if not WIDE:
        return np.ones(k)
    levels = np.array([10, -10, 5, -5, 0])
    if k % 512:
        return np.exp2(np.random.permutation(np.resize(levels, k // 32))).repeat(32)
    a = np.empty((k // 512, 16))
    for p in range(k // 512):
        a[p, :8] = np.random.permutation(np.resize(levels, 8))
        for g in range(8):
            far = levels[np.abs(levels - a[p, g]) >= 10]
            a[p, g + 8] = far[np.random.randint(len(far))]
    return np.exp2(a.ravel()).repeat(32)


def f64(x):
    return np.asarray(x).astype(np.float64)


def striped(idx):
    return np.tile(idx.reshape(-1, 16).T, (8, 1)).astype(np.uint16)


def unstriped(offs):
    return offs[:16].T.reshape(-1).astype(np.int64)


def pack_weight(w):
    k, n = w.shape
    w = f64(np.asarray(w, np.float32).astype(ml_dtypes.bfloat16)).reshape(k // 32, 32, n)
    amax = np.abs(w).max(1)
    byte = np.clip(np.where(amax > 0, np.frexp(amax)[1] - 1 + 127 - 7, 1), 1, 254)
    scaled = (w * np.exp2(127.0 - byte)[:, None, :]).reshape(k, n).astype(np.float32)
    words = np.ascontiguousarray(scaled.reshape(k // 512, 128, 4, n).transpose(0, 1, 3, 2)).astype(ml_dtypes.float8_e4m3fn).view(np.uint8)
    return words, np.ascontiguousarray(byte.astype(np.uint8).reshape(k // 512, 16, n))


def unpack_weight(words, scales):
    g, p, n, _ = words.shape
    vals = np.ascontiguousarray(words).view(ml_dtypes.float8_e4m3fn).astype(np.float64) * np.repeat(np.exp2(scales.astype(np.float64) - 127.0), 8, axis=1)[..., None]
    return vals.transpose(0, 1, 3, 2).reshape(g * 512, n)


def relu2(v):
    return np.maximum(v, 0.0) ** 2


K, T, D, S, V, N = 512, 2048, 3, 1024, 512, 128


def setup_inputs():
    n = np.random.standard_normal
    s = mx_kscale(K)[:, None]
    packed = pack_weight(n((K, T)) * s)
    return {
        "x_words": packed[0],
        "x_scales": packed[1],
        "w": (n((K, N)) / np.sqrt(K) / s).astype(np.float32),
        "b": (0.3 * n((N, 1))).astype(np.float32),
        "gate": np.tile(np.random.uniform(0.2, 1.0, (D, 1, V)) / np.sqrt(D), (1, N, 1)).astype(np.float32),
        "offs": striped(np.random.permutation(T)[:S]),
        "pos1": striped(np.random.permutation(S)[:V]),
        "pos2": striped(np.random.permutation(S)[:V]),
        "pos3": striped(np.random.permutation(S)[:V]),
    }


def reference(x_words, x_scales, w, b, gate, offs, pos1, pos2, pos3):
    idx = unstriped(offs)
    xq = unpack_weight(x_words, x_scales)[:, idx]
    y = mxq(f64(w), 0, "e4m3").T @ xq
    y = relu2(y + f64(b))
    return sum(f64(gate[d]) * y[:, unstriped(p)] for d, p in enumerate((pos1, pos2, pos3)))

@@ -1,0 +1,94 @@
+from contextlib import ExitStack
+
+import concourse.mybir as mybir
+
+K, T, D, S, V, N = 512, 2048, 3, 1024, 512, 128
+FLOPS = 2 * K * S * N
+
+F32 = mybir.dt.float32
+BF16 = mybir.dt.bfloat16
+I32 = mybir.dt.int32
+U32 = mybir.dt.uint32
+U16 = mybir.dt.uint16
+U8 = mybir.dt.uint8
+FP8X4 = mybir.dt.float8_e4m3fn_x4
+ACT = mybir.ActivationFunctionType
+ALU = mybir.AluOpType
+
+P = 128
+PACK = 4
+LANES = 16
+CHUNK = 256
+
+
+def tile_picked_sub_lin_relu2_sub_p_kernel(tc, x_words, x_scales, w, b, gate, offs, pos1, pos2, pos3, out):
+    nc = tc.nc
+    with ExitStack() as ctx:
+        keep = ctx.enter_context(tc.tile_pool(name="keep", bufs=1))
+        psum = ctx.enter_context(tc.psum_pool(name="psum", bufs=1))
+
+        offs_sb = keep.tile([P, S // LANES], U16, name="offs_sb")
+        pos_sb = [keep.tile([P, V // LANES], U16, name="pos_sb%d" % d) for d in range(D)]
+        scale_store = keep.tile([P, T // 4], I32, name="scale_store", align_bytes=64)
+        word_store = keep.tile([P, T], I32, name="word_store", align_bytes=64)
+        w_raw = keep.tile([P, PACK, N], F32, name="w_raw")
+        w_bf = keep.tile([P, N, PACK], BF16, name="w_bf", align_bytes=64)
+        w_codes = keep.tile([P, N], U32, name="w_codes", align_bytes=64)
+        w_scales = keep.tile([P, N], U8, name="w_scales", align_bytes=64)
+        bias = keep.tile([P, 1], F32, name="bias")
+        gate_sb = keep.tile([P, D, V], F32, name="gate_sb")
+        picked_words = keep.tile([P, S], U32, name="picked_words", align_bytes=64)
+        picked_scales = keep.tile([P, S], U8, name="picked_scales", align_bytes=64)
+        rect = keep.tile([P, S], F32, name="rect")
+        y = keep.tile([P, S], F32, name="y")
+        terms = keep.tile([P, D, V], F32, name="terms")
+        pair = keep.tile([P, V], F32, name="pair")
+        total = keep.tile([P, V], F32, name="total")
+
+        nc.vector.memset(scale_store[:], 0)
+        nc.sync.dma_start(offs_sb[:], offs)
+        nc.sync.dma_start(w_raw[:], w.rearrange("(p j) n -> p j n", j=PACK))
+        for q in (0, 2, 1, 3):
+            nc.sync.dma_start(scale_store[32 * q : 32 * q + 4, :], x_scales[0, 4 * q : 4 * q + 4, :].bitcast(I32))
+        nc.sync.dma_start(word_store[:], x_words[0].rearrange("p c r -> p (c r)").bitcast(I32))
+        nc.sync.dma_start(bias[:], b)
+        for d, pos in enumerate((pos1, pos2, pos3)):
+            nc.sync.dma_start(pos_sb[d][:], pos)
+        nc.sync.dma_start(gate_sb[:], gate.rearrange("d p v -> p d v"))
+
+        nc.vector.tensor_copy(picked_scales[:], scale_store[:].bitcast(U8).indirect(offs_sb[:]))
+        nc.scalar.activation(w_bf[:], w_raw[:].rearrange("p j n -> p n j"), ACT.Copy)
+        nc.vector.quantize_mx(w_codes[:].bitcast(FP8X4), w_scales[:], w_bf[:].rearrange("p n j -> p (n j)"))
+
+        for c0 in range(0, S, CHUNK):
+            nc.vector.tensor_copy(
+                picked_words[:, c0 : c0 + CHUNK],
+                word_store[:].bitcast(U32).indirect(offs_sb[:, c0 // LANES : (c0 + CHUNK) // LANES]),
+            )
+        pieces = [(0, 256), (256, 256), (512, 256), (768, 128), (896, 128)]
+        for i, (c0, width) in enumerate(pieces):
+            cols = slice(c0, c0 + width)
+            acc = psum.tile([P, width], F32, name="acc%d" % i)
+            nc.tensor.matmul_mx(
+                out=acc[:],
+                lhsT=w_codes[:].bitcast(FP8X4),
+                lhsT_scale=w_scales[:],
+                rhs=picked_words[:, cols].bitcast(FP8X4),
+                rhs_scale=picked_scales[:, cols],
+                start=True,
+                stop=True,
+            )
+            nc.scalar.activation(rect[:, cols], acc[:], ACT.Relu, bias=bias[:])
+            if i == 0:
+                nc.scalar.activation(y[:, cols], rect[:, cols], ACT.Square)
+            else:
+                nc.vector.tensor_tensor(y[:, cols], rect[:, cols], rect[:, cols], ALU.mult)
+
+        for d in range(D):
+            nc.vector.tensor_tensor(terms[:, d, :], y[:].indirect(pos_sb[d][:]), gate_sb[:, d, :], ALU.mult)
+        halves = [slice(0, V // 2), slice(V // 2, V)]
+        for cols in halves:
+            nc.vector.tensor_tensor(pair[:, cols], terms[:, 0, cols], terms[:, 1, cols], ALU.add)
+        for cols in halves:
+            nc.vector.tensor_tensor(total[:, cols], pair[:, cols], terms[:, 2, cols], ALU.add)
+            nc.sync.dma_start(out[:, cols], total[:, cols])

@@ -48,8 +48,8 @@ def tile_picked_sub_lin_relu2_sub_p_kernel(tc, x_words, x_scales, w, b, gate, of
         nc.vector.memset(scale_store[:], 0)
         nc.sync.dma_start(offs_sb[:], offs)
         nc.sync.dma_start(w_raw[:], w.rearrange("(p j) n -> p j n", j=PACK))
-        for q in (0, 2, 1, 3):
-            nc.sync.dma_start(scale_store[32 * q : 32 * q + 4, :], x_scales[0, 4 * q : 4 * q + 4, :].bitcast(I32))
+        for q, queue in ((0, nc.sync), (2, nc.scalar), (3, nc.sync), (1, nc.scalar)):
+            queue.dma_start(scale_store[32 * q : 32 * q + 4, :], x_scales[0, 4 * q : 4 * q + 4, :].bitcast(I32))
         nc.sync.dma_start(word_store[:], x_words[0].rearrange("p c r -> p (c r)").bitcast(I32))
         nc.sync.dma_start(bias[:], b)
         for d, pos in enumerate((pos1, pos2, pos3)):
@@ -60,26 +60,32 @@ def tile_picked_sub_lin_relu2_sub_p_kernel(tc, x_words, x_scales, w, b, gate, of
         nc.scalar.activation(w_bf[:], w_raw[:].rearrange("p j n -> p n j"), ACT.Copy)
         nc.vector.quantize_mx(w_codes[:].bitcast(FP8X4), w_scales[:], w_bf[:].rearrange("p n j -> p (n j)"))
 
-        for c0 in range(0, S, CHUNK):
+        for c0, c1 in ((0, 512), (512, 768), (768, 1024)):
             nc.vector.tensor_copy(
-                picked_words[:, c0 : c0 + CHUNK],
-                word_store[:].bitcast(U32).indirect(offs_sb[:, c0 // LANES : (c0 + CHUNK) // LANES]),
+                picked_words[:, c0:c1],
+                word_store[:].bitcast(U32).indirect(offs_sb[:, c0 // LANES : c1 // LANES]),
             )
-        pieces = [(0, 256), (256, 256), (512, 256), (768, 128), (896, 128)]
-        for i, (c0, width) in enumerate(pieces):
-            cols = slice(c0, c0 + width)
-            acc = psum.tile([P, width], F32, name="acc%d" % i)
+        pieces = ((0, 256), (256, 512), (512, 768), (768, 896), (896, 1024))
+        accs = []
+        for i, (c0, c1) in enumerate(pieces):
+            acc = psum.tile([P, c1 - c0], F32, name="acc%d" % i)
+            accs.append(acc)
             nc.tensor.matmul_mx(
                 out=acc[:],
                 lhsT=w_codes[:].bitcast(FP8X4),
                 lhsT_scale=w_scales[:],
-                rhs=picked_words[:, cols].bitcast(FP8X4),
-                rhs_scale=picked_scales[:, cols],
+                rhs=picked_words[:, c0:c1].bitcast(FP8X4),
+                rhs_scale=picked_scales[:, c0:c1],
                 start=True,
                 stop=True,
             )
-            nc.scalar.activation(rect[:, cols], acc[:], ACT.Relu, bias=bias[:])
-            if i == 0:
+        for step, engine, i in [("r", "s", 0), ("r", "s", 1), ("q", "s", 0), ("r", "s", 2), ("q", "v", 1), ("q", "v", 2), ("r", "s", 3), ("r", "s", 4), ("q", "v", 3), ("q", "v", 4)]:
+            cols = slice(pieces[i][0], pieces[i][1])
+            if step == "r" and engine == "s":
+                nc.scalar.activation(rect[:, cols], accs[i][:], ACT.Relu, bias=bias[:])
+            elif step == "r":
+                nc.vector.tensor_scalar(rect[:, cols], accs[i][:], bias[:], 0.0, ALU.add, ALU.max)
+            elif engine == "s":
                 nc.scalar.activation(y[:, cols], rect[:, cols], ACT.Square)
             else:
                 nc.vector.tensor_tensor(y[:, cols], rect[:, cols], rect[:, cols], ALU.mult)

@@ -47,13 +47,14 @@ def tile_picked_sub_lin_relu2_sub_p_kernel(tc, x_words, x_scales, w, b, gate, of
 
         nc.vector.memset(scale_store[:], 0)
         nc.sync.dma_start(offs_sb[:], offs)
+        nc.sync.dma_start(pos_sb[0][:], pos1)
+        for r in range(4):
+            nc.sync.dma_start(scale_store[r:P:32, :], x_scales[0, r:16:4, :].bitcast(I32))
         nc.sync.dma_start(w_raw[:], w.rearrange("(p j) n -> p j n", j=PACK))
-        for q, queue in ((0, nc.sync), (2, nc.scalar), (3, nc.sync), (1, nc.scalar)):
-            queue.dma_start(scale_store[32 * q : 32 * q + 4, :], x_scales[0, 4 * q : 4 * q + 4, :].bitcast(I32))
         nc.sync.dma_start(word_store[:], x_words[0].rearrange("p c r -> p (c r)").bitcast(I32))
         nc.sync.dma_start(bias[:], b)
-        for d, pos in enumerate((pos1, pos2, pos3)):
-            nc.sync.dma_start(pos_sb[d][:], pos)
+        nc.sync.dma_start(pos_sb[1][:], pos2)
+        nc.sync.dma_start(pos_sb[2][:], pos3)
         nc.sync.dma_start(gate_sb[:], gate.rearrange("d p v -> p d v"))
 
         nc.vector.tensor_copy(picked_scales[:], scale_store[:].bitcast(U8).indirect(offs_sb[:]))

@@ -18,7 +18,8 @@ ALU = mybir.AluOpType
 P = 128
 PACK = 4
 LANES = 16
-CHUNK = 256
+ROW0 = 112
+HALF = 512
 
 
 def tile_picked_sub_lin_relu2_sub_p_kernel(tc, x_words, x_scales, w, b, gate, offs, pos1, pos2, pos3, out):
@@ -29,35 +30,46 @@ def tile_picked_sub_lin_relu2_sub_p_kernel(tc, x_words, x_scales, w, b, gate, of
 
         offs_sb = keep.tile([P, S // LANES], U16, name="offs_sb")
         pos_sb = [keep.tile([P, V // LANES], U16, name="pos_sb%d" % d) for d in range(D)]
-        scale_store = keep.tile([P, T // 4], I32, name="scale_store", align_bytes=64)
+        scale_store = keep.tile([P, T // 4], I32, name="scale_store", tag="scale_then_gate", align_bytes=64)
         word_store = keep.tile([P, T], I32, name="word_store", align_bytes=64)
         w_raw = keep.tile([P, PACK, N], F32, name="w_raw")
         w_bf = keep.tile([P, N, PACK], BF16, name="w_bf", align_bytes=64)
         w_codes = keep.tile([P, N], U32, name="w_codes", align_bytes=64)
         w_scales = keep.tile([P, N], U8, name="w_scales", align_bytes=64)
         bias = keep.tile([P, 1], F32, name="bias")
-        gate_sb = keep.tile([P, D, V], F32, name="gate_sb")
         picked_words = keep.tile([P, S], U32, name="picked_words", align_bytes=64)
-        picked_scales = keep.tile([P, S], U8, name="picked_scales", align_bytes=64)
+        picked_rows = [keep.tile([P, HALF], U8, name="picked_rows%d" % h, align_bytes=64) for h in range(2)]
+        picked_scales = [keep.tile([P, HALF], U8, name="picked_scales%d" % h, align_bytes=64) for h in range(2)]
         rect = keep.tile([P, S], F32, name="rect")
         y = keep.tile([P, S], F32, name="y")
         terms = keep.tile([P, D, V], F32, name="terms")
         pair = keep.tile([P, V], F32, name="pair")
         total = keep.tile([P, V], F32, name="total")
 
-        nc.vector.memset(scale_store[:], 0)
+        nc.vector.memset(scale_store[0:ROW0, :], 0)
+        for h in range(2):
+            nc.vector.memset(picked_scales[h][:].bitcast(I32), 0)
+        nc.sync.dma_start(scale_store[ROW0:P, :], x_scales[0].bitcast(I32))
         nc.sync.dma_start(offs_sb[:], offs)
+        nc.sync.dma_start(bias[:], b)
         nc.sync.dma_start(pos_sb[0][:], pos1)
-        for r in range(4):
-            nc.sync.dma_start(scale_store[r:P:32, :], x_scales[0, r:16:4, :].bitcast(I32))
         nc.sync.dma_start(w_raw[:], w.rearrange("(p j) n -> p j n", j=PACK))
         nc.sync.dma_start(word_store[:], x_words[0].rearrange("p c r -> p (c r)").bitcast(I32))
-        nc.sync.dma_start(bias[:], b)
         nc.sync.dma_start(pos_sb[1][:], pos2)
         nc.sync.dma_start(pos_sb[2][:], pos3)
-        nc.sync.dma_start(gate_sb[:], gate.rearrange("d p v -> p d v"))
 
-        nc.vector.tensor_copy(picked_scales[:], scale_store[:].bitcast(U8).indirect(offs_sb[:]))
+        for h, (c0, c1) in enumerate(((0, 512), (512, 1024))):
+            nc.vector.tensor_copy(
+                picked_rows[h][:],
+                scale_store[:].bitcast(U8).indirect(offs_sb[:, c0 // LANES : c1 // LANES]),
+            )
+            for r in range(4):
+                nc.sync.dma_start(
+                    picked_scales[h][r:P:32, :].bitcast(I32),
+                    picked_rows[h][ROW0 + r : P : 4, :].bitcast(I32),
+                )
+        gate_sb = keep.tile([P, D, V], F32, name="gate_sb", tag="scale_then_gate", align_bytes=64)
+        nc.sync.dma_start(gate_sb[:], gate.rearrange("d p v -> p d v"))
         nc.scalar.activation(w_bf[:], w_raw[:].rearrange("p j n -> p n j"), ACT.Copy)
         nc.vector.quantize_mx(w_codes[:].bitcast(FP8X4), w_scales[:], w_bf[:].rearrange("p n j -> p (n j)"))
 
@@ -76,7 +88,7 @@ def tile_picked_sub_lin_relu2_sub_p_kernel(tc, x_words, x_scales, w, b, gate, of
                 lhsT=w_codes[:].bitcast(FP8X4),
                 lhsT_scale=w_scales[:],
                 rhs=picked_words[:, c0:c1].bitcast(FP8X4),
-                rhs_scale=picked_scales[:, c0:c1],
+                rhs_scale=picked_scales[c0 // HALF][:, c0 % HALF : c0 % HALF + c1 - c0],
                 start=True,
                 stop=True,
             )

@@ -18,8 +18,18 @@ ALU = mybir.AluOpType
 P = 128
 PACK = 4
 LANES = 16
-ROW0 = 112
-HALF = 512
+QUADRANT = 32
+ROWS_PER_QUADRANT = 4
+SCALE_ROWS = K // 32
+ROW0 = P - SCALE_ROWS
+HALF = S // 2
+
+WORD_GATHERS = ((0, 512), (512, 768), (768, 1024))
+PIECES = ((0, 256), (256, 512), (512, 768), (768, 896), (896, 1024))
+
+
+def entries(list_tile, c0, c1):
+    return list_tile[:, c0 // LANES : c1 // LANES]
 
 
 def tile_picked_sub_lin_relu2_sub_p_kernel(tc, x_words, x_scales, w, b, gate, offs, pos1, pos2, pos3, out):
@@ -39,7 +49,7 @@ def tile_picked_sub_lin_relu2_sub_p_kernel(tc, x_words, x_scales, w, b, gate, of
         bias = keep.tile([P, 1], F32, name="bias")
         picked_words = keep.tile([P, S], U32, name="picked_words", align_bytes=64)
         picked_rows = [keep.tile([P, HALF], U8, name="picked_rows%d" % h, align_bytes=64) for h in range(2)]
-        picked_scales = [keep.tile([P, HALF], U8, name="picked_scales%d" % h, align_bytes=64) for h in range(2)]
+        planes = [keep.tile([P, HALF], U8, name="planes%d" % h, align_bytes=64) for h in range(2)]
         rect = keep.tile([P, S], F32, name="rect")
         y = keep.tile([P, S], F32, name="y")
         terms = keep.tile([P, D, V], F32, name="terms")
@@ -47,8 +57,9 @@ def tile_picked_sub_lin_relu2_sub_p_kernel(tc, x_words, x_scales, w, b, gate, of
         total = keep.tile([P, V], F32, name="total")
 
         nc.vector.memset(scale_store[0:ROW0, :], 0)
-        for h in range(2):
-            nc.vector.memset(picked_scales[h][:].bitcast(I32), 0)
+        for plane in planes:
+            nc.vector.memset(plane[:].bitcast(I32), 0)
+
         nc.sync.dma_start(scale_store[ROW0:P, :], x_scales[0].bitcast(I32))
         nc.sync.dma_start(offs_sb[:], offs)
         nc.sync.dma_start(bias[:], b)
@@ -58,56 +69,57 @@ def tile_picked_sub_lin_relu2_sub_p_kernel(tc, x_words, x_scales, w, b, gate, of
         nc.sync.dma_start(pos_sb[1][:], pos2)
         nc.sync.dma_start(pos_sb[2][:], pos3)
 
-        for h, (c0, c1) in enumerate(((0, 512), (512, 1024))):
+        for h in range(2):
             nc.vector.tensor_copy(
                 picked_rows[h][:],
-                scale_store[:].bitcast(U8).indirect(offs_sb[:, c0 // LANES : c1 // LANES]),
+                scale_store[:].bitcast(U8).indirect(entries(offs_sb, h * HALF, (h + 1) * HALF)),
             )
-            for r in range(4):
+            for r in range(ROWS_PER_QUADRANT):
                 nc.sync.dma_start(
-                    picked_scales[h][r:P:32, :].bitcast(I32),
-                    picked_rows[h][ROW0 + r : P : 4, :].bitcast(I32),
+                    planes[h][r:P:QUADRANT, :].bitcast(I32),
+                    picked_rows[h][ROW0 + r : P : ROWS_PER_QUADRANT, :].bitcast(I32),
                 )
+
         gate_sb = keep.tile([P, D, V], F32, name="gate_sb", tag="scale_then_gate", align_bytes=64)
-        nc.sync.dma_start(gate_sb[:], gate.rearrange("d p v -> p d v"))
+        for d in range(D):
+            nc.sync.dma_start(gate_sb[:, d, :], gate[d])
+
         nc.scalar.activation(w_bf[:], w_raw[:].rearrange("p j n -> p n j"), ACT.Copy)
         nc.vector.quantize_mx(w_codes[:].bitcast(FP8X4), w_scales[:], w_bf[:].rearrange("p n j -> p (n j)"))
 
-        for c0, c1 in ((0, 512), (512, 768), (768, 1024)):
-            nc.vector.tensor_copy(
-                picked_words[:, c0:c1],
-                word_store[:].bitcast(U32).indirect(offs_sb[:, c0 // LANES : c1 // LANES]),
-            )
-        pieces = ((0, 256), (256, 512), (512, 768), (768, 896), (896, 1024))
+        for c0, c1 in WORD_GATHERS:
+            nc.vector.tensor_copy(picked_words[:, c0:c1], word_store[:].bitcast(U32).indirect(entries(offs_sb, c0, c1)))
+
         accs = []
-        for i, (c0, c1) in enumerate(pieces):
+        for i, (c0, c1) in enumerate(PIECES):
             acc = psum.tile([P, c1 - c0], F32, name="acc%d" % i)
             accs.append(acc)
+            in_half = c0 % HALF
             nc.tensor.matmul_mx(
                 out=acc[:],
                 lhsT=w_codes[:].bitcast(FP8X4),
                 lhsT_scale=w_scales[:],
                 rhs=picked_words[:, c0:c1].bitcast(FP8X4),
-                rhs_scale=picked_scales[c0 // HALF][:, c0 % HALF : c0 % HALF + c1 - c0],
+                rhs_scale=planes[c0 // HALF][:, in_half : in_half + c1 - c0],
                 start=True,
                 stop=True,
             )
-        for step, engine, i in [("r", "s", 0), ("r", "s", 1), ("q", "s", 0), ("r", "s", 2), ("q", "v", 1), ("q", "v", 2), ("r", "s", 3), ("r", "s", 4), ("q", "v", 3), ("q", "v", 4)]:
-            cols = slice(pieces[i][0], pieces[i][1])
-            if step == "r" and engine == "s":
-                nc.scalar.activation(rect[:, cols], accs[i][:], ACT.Relu, bias=bias[:])
-            elif step == "r":
-                nc.vector.tensor_scalar(rect[:, cols], accs[i][:], bias[:], 0.0, ALU.add, ALU.max)
-            elif engine == "s":
-                nc.scalar.activation(y[:, cols], rect[:, cols], ACT.Square)
-            else:
-                nc.vector.tensor_tensor(y[:, cols], rect[:, cols], rect[:, cols], ALU.mult)
+
+        piece_cols = [slice(c0, c1) for c0, c1 in PIECES]
+        first_gather_pieces = WORD_GATHERS[0][1] // PIECES[0][1]
+        for i, cols in enumerate(piece_cols):
+            nc.scalar.activation(rect[:, cols], accs[i][:], ACT.Relu, bias=bias[:])
+            if i == first_gather_pieces - 1:
+                nc.scalar.activation(y[:, piece_cols[0]], rect[:, piece_cols[0]], ACT.Square)
+        for cols in piece_cols[1:]:
+            nc.vector.tensor_tensor(y[:, cols], rect[:, cols], rect[:, cols], ALU.mult)
 
         for d in range(D):
             nc.vector.tensor_tensor(terms[:, d, :], y[:].indirect(pos_sb[d][:]), gate_sb[:, d, :], ALU.mult)
-        halves = [slice(0, V // 2), slice(V // 2, V)]
-        for cols in halves:
+
+        target_halves = [slice(0, V // 2), slice(V // 2, V)]
+        for cols in target_halves:
             nc.vector.tensor_tensor(pair[:, cols], terms[:, 0, cols], terms[:, 1, cols], ALU.add)
-        for cols in halves:
+        for cols in target_halves:
             nc.vector.tensor_tensor(total[:, cols], pair[:, cols], terms[:, 2, cols], ALU.add)
             nc.sync.dma_start(out[:, cols], total[:, cols])

@@ -120,6 +120,6 @@ def tile_picked_sub_lin_relu2_sub_p_kernel(tc, x_words, x_scales, w, b, gate, of
         target_halves = [slice(0, V // 2), slice(V // 2, V)]
         for cols in target_halves:
             nc.vector.tensor_tensor(pair[:, cols], terms[:, 0, cols], terms[:, 1, cols], ALU.add)
-        for cols in target_halves:
+        for cols in (slice(0, V // 2), slice(V // 2, 3 * V // 4), slice(3 * V // 4, V)):
             nc.vector.tensor_tensor(total[:, cols], pair[:, cols], terms[:, 2, cols], ALU.add)
             nc.sync.dma_start(out[:, cols], total[:, cols])

@@ -1,6 +1,7 @@
 from contextlib import ExitStack
 
 import concourse.mybir as mybir
+from concourse.masks import make_identity
 
 K, T, D, S, V, N = 512, 2048, 3, 1024, 512, 128
 FLOPS = 2 * K * S * N
@@ -22,10 +23,11 @@ QUADRANT = 32
 ROWS_PER_QUADRANT = 4
 SCALE_ROWS = K // 32
 ROW0 = P - SCALE_ROWS
-HALF = S // 2
+SCALE_PARTS = ((0, 640), (640, S))
 
 WORD_GATHERS = ((0, 512), (512, 768), (768, 1024))
-PIECES = ((0, 256), (256, 512), (512, 768), (768, 896), (896, 1024))
+PIECES = ((0, 256), (256, 512), (512, 640), (640, 768), (768, 896), (896, 1024))
+TURNED_BLOCKS = 3
 
 
 def entries(list_tile, c0, c1):
@@ -48,31 +50,35 @@ def tile_picked_sub_lin_relu2_sub_p_kernel(tc, x_words, x_scales, w, b, gate, of
         w_scales = keep.tile([P, N], U8, name="w_scales", align_bytes=64)
         bias = keep.tile([P, 1], F32, name="bias")
         picked_words = keep.tile([P, S], U32, name="picked_words", align_bytes=64)
-        picked_rows = [keep.tile([P, HALF], U8, name="picked_rows%d" % h, align_bytes=64) for h in range(2)]
-        planes = [keep.tile([P, HALF], U8, name="planes%d" % h, align_bytes=64) for h in range(2)]
+        picked_rows = [keep.tile([P, c1 - c0], U8, name="picked_rows%d" % h, align_bytes=64) for h, (c0, c1) in enumerate(SCALE_PARTS)]
+        planes = [keep.tile([P, c1 - c0], U8, name="planes%d" % h, align_bytes=64) for h, (c0, c1) in enumerate(SCALE_PARTS)]
         rect = keep.tile([P, S], F32, name="rect")
         y = keep.tile([P, S], F32, name="y")
         terms = keep.tile([P, D, V], F32, name="terms")
-        pair = keep.tile([P, V], F32, name="pair")
+        ident = keep.tile([P, P], F32, name="ident")
+        turned = [keep.tile([P, P], F32, name="turned%d" % j) for j in range(TURNED_BLOCKS)]
+        pair_last = keep.tile([P, P], F32, name="pair_last")
         total = keep.tile([P, V], F32, name="total")
 
         nc.vector.memset(scale_store[0:ROW0, :], 0)
         for plane in planes:
             nc.vector.memset(plane[:].bitcast(I32), 0)
 
-        nc.sync.dma_start(scale_store[ROW0:P, :], x_scales[0].bitcast(I32))
+        make_identity(nc, ident[:])
+
+        nc.scalar.dma_start(scale_store[ROW0:P, :], x_scales[0].bitcast(I32))
         nc.sync.dma_start(offs_sb[:], offs)
-        nc.sync.dma_start(bias[:], b)
-        nc.sync.dma_start(pos_sb[0][:], pos1)
+        nc.gpsimd.dma_start(bias[:], b)
         nc.sync.dma_start(w_raw[:], w.rearrange("(p j) n -> p j n", j=PACK))
         nc.sync.dma_start(word_store[:], x_words[0].rearrange("p c r -> p (c r)").bitcast(I32))
+        nc.sync.dma_start(pos_sb[0][:], pos1)
         nc.sync.dma_start(pos_sb[1][:], pos2)
         nc.sync.dma_start(pos_sb[2][:], pos3)
 
-        for h in range(2):
+        for h, (c0, c1) in enumerate(SCALE_PARTS):
             nc.vector.tensor_copy(
                 picked_rows[h][:],
-                scale_store[:].bitcast(U8).indirect(entries(offs_sb, h * HALF, (h + 1) * HALF)),
+                scale_store[:].bitcast(U8).indirect(entries(offs_sb, c0, c1)),
             )
             for r in range(ROWS_PER_QUADRANT):
                 nc.sync.dma_start(
@@ -92,15 +98,16 @@ def tile_picked_sub_lin_relu2_sub_p_kernel(tc, x_words, x_scales, w, b, gate, of
 
         accs = []
         for i, (c0, c1) in enumerate(PIECES):
-            acc = psum.tile([P, c1 - c0], F32, name="acc%d" % i)
+            acc = psum.tile([P, c1 - c0], F32, name="acc%d" % i, tag="bank%d" % i)
             accs.append(acc)
-            in_half = c0 % HALF
+            part = 0 if c0 < SCALE_PARTS[1][0] else 1
+            in_part = c0 - SCALE_PARTS[part][0]
             nc.tensor.matmul_mx(
                 out=acc[:],
                 lhsT=w_codes[:].bitcast(FP8X4),
                 lhsT_scale=w_scales[:],
                 rhs=picked_words[:, c0:c1].bitcast(FP8X4),
-                rhs_scale=planes[c0 // HALF][:, in_half : in_half + c1 - c0],
+                rhs_scale=planes[part][:, in_part : in_part + c1 - c0],
                 start=True,
                 stop=True,
             )
@@ -114,12 +121,29 @@ def tile_picked_sub_lin_relu2_sub_p_kernel(tc, x_words, x_scales, w, b, gate, of
         for cols in piece_cols[1:]:
             nc.vector.tensor_tensor(y[:, cols], rect[:, cols], rect[:, cols], ALU.mult)
 
-        for d in range(D):
-            nc.vector.tensor_tensor(terms[:, d, :], y[:].indirect(pos_sb[d][:]), gate_sb[:, d, :], ALU.mult)
+        split = TURNED_BLOCKS * P
+        for d, c0, c1 in ((0, 0, split), (1, 0, split), (0, split, V), (1, split, V), (2, 0, V)):
+            nc.vector.tensor_tensor(terms[:, d, c0:c1], y[:].indirect(entries(pos_sb[d], c0, c1)), gate_sb[:, d, c0:c1], ALU.mult)
 
-        target_halves = [slice(0, V // 2), slice(V // 2, V)]
-        for cols in target_halves:
-            nc.vector.tensor_tensor(pair[:, cols], terms[:, 0, cols], terms[:, 1, cols], ALU.add)
-        for cols in (slice(0, V // 2), slice(V // 2, 3 * V // 4), slice(3 * V // 4, V)):
-            nc.vector.tensor_tensor(total[:, cols], pair[:, cols], terms[:, 2, cols], ALU.add)
+        blocks = [slice(j * P, (j + 1) * P) for j in range(TURNED_BLOCKS)]
+        sums_t = [psum.tile([P, P], F32, name="sum_t%d" % j, tag="bank%d" % j) for j in range(TURNED_BLOCKS)]
+        for d in range(2):
+            for j, cols in enumerate(blocks):
+                nc.tensor.matmul(sums_t[j][:], terms[:, d, cols], ident[:], start=(d == 0), stop=(d == 1), is_transpose=True)
+        for j in range(TURNED_BLOCKS):
+            nc.scalar.copy(turned[j][:], sums_t[j][:])
+        first = psum.tile([P, 2 * P], F32, name="pair_first", tag="bank3")
+        third = psum.tile([P, P], F32, name="pair_third", tag="bank4")
+        for j, dst in enumerate((first[:, 0:P], first[:, P : 2 * P], third[:])):
+            nc.tensor.transpose(dst, turned[j][:], ident[:])
+        last0 = TURNED_BLOCKS * P
+        for h in range(2):
+            cols = slice(last0 + h * P // 2, last0 + (h + 1) * P // 2)
+            nc.vector.tensor_tensor(pair_last[:, h * P // 2 : (h + 1) * P // 2], terms[:, 0, cols], terms[:, 1, cols], ALU.add)
+        for h in range(2):
+            cols = slice(last0 + h * P // 2, last0 + (h + 1) * P // 2)
+            nc.vector.tensor_tensor(total[:, cols], pair_last[:, h * P // 2 : (h + 1) * P // 2], terms[:, 2, cols], ALU.add)
+        nc.sync.dma_start(out[:, last0:V], total[:, last0:V])
+        for pair, cols in ((first, slice(0, 2 * P)), (third, blocks[2])):
+            nc.vector.tensor_tensor(total[:, cols], pair[:], terms[:, 2, cols], ALU.add)
             nc.sync.dma_start(out[:, cols], total[:, cols])

@@ -27,7 +27,7 @@ SCALE_PARTS = ((0, 640), (640, S))
 
 WORD_GATHERS = ((0, 512), (512, 768), (768, 1024))
 PIECES = ((0, 256), (256, 512), (512, 640), (640, 768), (768, 896), (896, 1024))
-TURNED_BLOCKS = 3
+TURNED_BLOCKS = 2
 
 
 def entries(list_tile, c0, c1):
@@ -57,7 +57,7 @@ def tile_picked_sub_lin_relu2_sub_p_kernel(tc, x_words, x_scales, w, b, gate, of
         terms = keep.tile([P, D, V], F32, name="terms")
         ident = keep.tile([P, P], F32, name="ident")
         turned = [keep.tile([P, P], F32, name="turned%d" % j) for j in range(TURNED_BLOCKS)]
-        pair_last = keep.tile([P, P], F32, name="pair_last")
+        own_pairs = [keep.tile([P, P], F32, name="own_pair%d" % j) for j in range(V // P - TURNED_BLOCKS)]
         total = keep.tile([P, V], F32, name="total")
 
         nc.vector.memset(scale_store[0:ROW0, :], 0)
@@ -121,29 +121,30 @@ def tile_picked_sub_lin_relu2_sub_p_kernel(tc, x_words, x_scales, w, b, gate, of
         for cols in piece_cols[1:]:
             nc.vector.tensor_tensor(y[:, cols], rect[:, cols], rect[:, cols], ALU.mult)
 
-        split = TURNED_BLOCKS * P
-        for d, c0, c1 in ((0, 0, split), (1, 0, split), (0, split, V), (1, split, V), (2, 0, V)):
-            nc.vector.tensor_tensor(terms[:, d, c0:c1], y[:].indirect(entries(pos_sb[d], c0, c1)), gate_sb[:, d, c0:c1], ALU.mult)
+        for d in range(D):
+            nc.vector.tensor_tensor(terms[:, d, :], y[:].indirect(pos_sb[d][:]), gate_sb[:, d, :], ALU.mult)
 
-        blocks = [slice(j * P, (j + 1) * P) for j in range(TURNED_BLOCKS)]
+        target_blocks = [slice(j * P, (j + 1) * P) for j in range(V // P)]
         sums_t = [psum.tile([P, P], F32, name="sum_t%d" % j, tag="bank%d" % j) for j in range(TURNED_BLOCKS)]
         for d in range(2):
-            for j, cols in enumerate(blocks):
-                nc.tensor.matmul(sums_t[j][:], terms[:, d, cols], ident[:], start=(d == 0), stop=(d == 1), is_transpose=True)
+            for j in range(TURNED_BLOCKS):
+                nc.tensor.matmul(
+                    sums_t[j][:], terms[:, d, target_blocks[j]], ident[:], start=(d == 0), stop=(d == 1), is_transpose=True
+                )
+        bank_pairs = []
         for j in range(TURNED_BLOCKS):
             nc.scalar.copy(turned[j][:], sums_t[j][:])
-        first = psum.tile([P, 2 * P], F32, name="pair_first", tag="bank3")
-        third = psum.tile([P, P], F32, name="pair_third", tag="bank4")
-        for j, dst in enumerate((first[:, 0:P], first[:, P : 2 * P], third[:])):
-            nc.tensor.transpose(dst, turned[j][:], ident[:])
-        last0 = TURNED_BLOCKS * P
-        for h in range(2):
-            cols = slice(last0 + h * P // 2, last0 + (h + 1) * P // 2)
-            nc.vector.tensor_tensor(pair_last[:, h * P // 2 : (h + 1) * P // 2], terms[:, 0, cols], terms[:, 1, cols], ALU.add)
-        for h in range(2):
-            cols = slice(last0 + h * P // 2, last0 + (h + 1) * P // 2)
-            nc.vector.tensor_tensor(total[:, cols], pair_last[:, h * P // 2 : (h + 1) * P // 2], terms[:, 2, cols], ALU.add)
-        nc.sync.dma_start(out[:, last0:V], total[:, last0:V])
-        for pair, cols in ((first, slice(0, 2 * P)), (third, blocks[2])):
+            pair = psum.tile([P, P], F32, name="pair%d" % j, tag="bank%d" % (TURNED_BLOCKS + j))
+            nc.tensor.transpose(pair[:], turned[j][:], ident[:])
+            bank_pairs.append(pair)
+
+        own_blocks = target_blocks[TURNED_BLOCKS:]
+        for pair, cols in zip(own_pairs, own_blocks):
+            nc.vector.tensor_tensor(pair[:], terms[:, 0, cols], terms[:, 1, cols], ALU.add)
+        for pair, cols in zip(own_pairs, own_blocks):
+            nc.vector.tensor_tensor(total[:, cols], pair[:], terms[:, 2, cols], ALU.add)
+        own_cols = slice(TURNED_BLOCKS * P, V)
+        nc.sync.dma_start(out[:, own_cols], total[:, own_cols])
+        for pair, cols in zip(bank_pairs, target_blocks):
             nc.vector.tensor_tensor(total[:, cols], pair[:], terms[:, 2, cols], ALU.add)
             nc.sync.dma_start(out[:, cols], total[:, cols])

@@ -25,7 +25,7 @@ SCALE_ROWS = K // 32
 ROW0 = P - SCALE_ROWS
 SCALE_PARTS = ((0, 640), (640, S))
 
-WORD_GATHERS = ((0, 512), (512, 768), (768, 1024))
+WORD_GATHERS = SCALE_PARTS
 PIECES = ((0, 256), (256, 512), (512, 640), (640, 768), (768, 896), (896, 1024))
 TURNED_BLOCKS = 2
 
@@ -44,12 +44,11 @@ def tile_picked_sub_lin_relu2_sub_p_kernel(tc, x_words, x_scales, w, b, gate, of
         pos_sb = [keep.tile([P, V // LANES], U16, name="pos_sb%d" % d) for d in range(D)]
         scale_store = keep.tile([P, T // 4], I32, name="scale_store", tag="scale_then_gate", align_bytes=64)
         word_store = keep.tile([P, T], I32, name="word_store", align_bytes=64)
-        w_raw = keep.tile([P, PACK, N], F32, name="w_raw")
+        w_raw = keep.tile([P, PACK, N], F32, name="w_raw", tag="w_then_words", align_bytes=64)
         w_bf = keep.tile([P, N, PACK], BF16, name="w_bf", align_bytes=64)
         w_codes = keep.tile([P, N], U32, name="w_codes", align_bytes=64)
         w_scales = keep.tile([P, N], U8, name="w_scales", align_bytes=64)
         bias = keep.tile([P, 1], F32, name="bias")
-        picked_words = keep.tile([P, S], U32, name="picked_words", align_bytes=64)
         picked_rows = [keep.tile([P, c1 - c0], U8, name="picked_rows%d" % h, align_bytes=64) for h, (c0, c1) in enumerate(SCALE_PARTS)]
         planes = [keep.tile([P, c1 - c0], U8, name="planes%d" % h, align_bytes=64) for h, (c0, c1) in enumerate(SCALE_PARTS)]
         rect = keep.tile([P, S], F32, name="rect")
@@ -69,11 +68,11 @@ def tile_picked_sub_lin_relu2_sub_p_kernel(tc, x_words, x_scales, w, b, gate, of
         nc.scalar.dma_start(scale_store[ROW0:P, :], x_scales[0].bitcast(I32))
         nc.sync.dma_start(offs_sb[:], offs)
         nc.gpsimd.dma_start(bias[:], b)
-        nc.sync.dma_start(w_raw[:], w.rearrange("(p j) n -> p j n", j=PACK))
         nc.sync.dma_start(word_store[:], x_words[0].rearrange("p c r -> p (c r)").bitcast(I32))
         nc.sync.dma_start(pos_sb[0][:], pos1)
         nc.sync.dma_start(pos_sb[1][:], pos2)
         nc.sync.dma_start(pos_sb[2][:], pos3)
+        nc.sync.dma_start(w_raw[:], w.rearrange("(p j) n -> p j n", j=PACK))
 
         for h, (c0, c1) in enumerate(SCALE_PARTS):
             nc.vector.tensor_copy(
@@ -90,11 +89,17 @@ def tile_picked_sub_lin_relu2_sub_p_kernel(tc, x_words, x_scales, w, b, gate, of
         for d in range(D):
             nc.sync.dma_start(gate_sb[:, d, :], gate[d])
 
-        nc.scalar.activation(w_bf[:], w_raw[:].rearrange("p j n -> p n j"), ACT.Copy)
+        nc.scalar.activation(
+            w_bf[:].rearrange("p (c i) j -> p c j i", i=PACK), w_raw[:].rearrange("p j (c i) -> p c j i", i=PACK), ACT.Copy
+        )
         nc.vector.quantize_mx(w_codes[:].bitcast(FP8X4), w_scales[:], w_bf[:].rearrange("p n j -> p (n j)"))
 
-        for c0, c1 in WORD_GATHERS:
-            nc.vector.tensor_copy(picked_words[:, c0:c1], word_store[:].bitcast(U32).indirect(entries(offs_sb, c0, c1)))
+        picked_words = [
+            keep.tile([P, SCALE_PARTS[0][1]], U32, name="picked_words0", align_bytes=64),
+            keep.tile([P, S - SCALE_PARTS[0][1]], U32, name="picked_words1", tag="w_then_words", align_bytes=64),
+        ]
+        for picked, (c0, c1) in zip(picked_words, WORD_GATHERS):
+            nc.vector.tensor_copy(picked[:], word_store[:].bitcast(U32).indirect(entries(offs_sb, c0, c1)))
 
         accs = []
         for i, (c0, c1) in enumerate(PIECES):
@@ -106,19 +111,16 @@ def tile_picked_sub_lin_relu2_sub_p_kernel(tc, x_words, x_scales, w, b, gate, of
                 out=acc[:],
                 lhsT=w_codes[:].bitcast(FP8X4),
                 lhsT_scale=w_scales[:],
-                rhs=picked_words[:, c0:c1].bitcast(FP8X4),
+                rhs=picked_words[part][:, in_part : in_part + c1 - c0].bitcast(FP8X4),
                 rhs_scale=planes[part][:, in_part : in_part + c1 - c0],
                 start=True,
                 stop=True,
             )
 
         piece_cols = [slice(c0, c1) for c0, c1 in PIECES]
-        first_gather_pieces = WORD_GATHERS[0][1] // PIECES[0][1]
         for i, cols in enumerate(piece_cols):
             nc.scalar.activation(rect[:, cols], accs[i][:], ACT.Relu, bias=bias[:])
-            if i == first_gather_pieces - 1:
-                nc.scalar.activation(y[:, piece_cols[0]], rect[:, piece_cols[0]], ACT.Square)
-        for cols in piece_cols[1:]:
+        for cols in piece_cols:
             nc.vector.tensor_tensor(y[:, cols], rect[:, cols], rect[:, cols], ALU.mult)
 
         for d in range(D):

@@ -21,11 +21,12 @@ PACK = 4
 LANES = 16
 QUADRANT = 32
 ROWS_PER_QUADRANT = 4
+HALF = S // 2
 SCALE_ROWS = K // 32
 ROW0 = P - SCALE_ROWS
 SCALE_PARTS = ((0, 640), (640, S))
 
-WORD_GATHERS = SCALE_PARTS
+WORD_GATHERS = ((0, 512), (512, 768), (768, 1024))
 PIECES = ((0, 256), (256, 512), (512, 640), (640, 768), (768, 896), (896, 1024))
 TURNED_BLOCKS = 2
 
@@ -69,10 +70,10 @@ def tile_picked_sub_lin_relu2_sub_p_kernel(tc, x_words, x_scales, w, b, gate, of
         nc.sync.dma_start(offs_sb[:], offs)
         nc.gpsimd.dma_start(bias[:], b)
         nc.sync.dma_start(word_store[:], x_words[0].rearrange("p c r -> p (c r)").bitcast(I32))
+        nc.sync.dma_start(w_raw[:], w.rearrange("(p j) n -> p j n", j=PACK))
         nc.sync.dma_start(pos_sb[0][:], pos1)
         nc.sync.dma_start(pos_sb[1][:], pos2)
         nc.sync.dma_start(pos_sb[2][:], pos3)
-        nc.sync.dma_start(w_raw[:], w.rearrange("(p j) n -> p j n", j=PACK))
 
         for h, (c0, c1) in enumerate(SCALE_PARTS):
             nc.vector.tensor_copy(
@@ -95,11 +96,14 @@ def tile_picked_sub_lin_relu2_sub_p_kernel(tc, x_words, x_scales, w, b, gate, of
         nc.vector.quantize_mx(w_codes[:].bitcast(FP8X4), w_scales[:], w_bf[:].rearrange("p n j -> p (n j)"))
 
         picked_words = [
-            keep.tile([P, SCALE_PARTS[0][1]], U32, name="picked_words0", align_bytes=64),
-            keep.tile([P, S - SCALE_PARTS[0][1]], U32, name="picked_words1", tag="w_then_words", align_bytes=64),
+            keep.tile([P, HALF], U32, name="picked_words0", align_bytes=64),
+            keep.tile([P, HALF], U32, name="picked_words1", tag="w_then_words", align_bytes=64),
         ]
-        for picked, (c0, c1) in zip(picked_words, WORD_GATHERS):
-            nc.vector.tensor_copy(picked[:], word_store[:].bitcast(U32).indirect(entries(offs_sb, c0, c1)))
+        for c0, c1 in WORD_GATHERS:
+            nc.vector.tensor_copy(
+                picked_words[c0 // HALF][:, c0 % HALF : c0 % HALF + c1 - c0],
+                word_store[:].bitcast(U32).indirect(entries(offs_sb, c0, c1)),
+            )
 
         accs = []
         for i, (c0, c1) in enumerate(PIECES):
@@ -111,7 +115,7 @@ def tile_picked_sub_lin_relu2_sub_p_kernel(tc, x_words, x_scales, w, b, gate, of
                 out=acc[:],
                 lhsT=w_codes[:].bitcast(FP8X4),
                 lhsT_scale=w_scales[:],
-                rhs=picked_words[part][:, in_part : in_part + c1 - c0].bitcast(FP8X4),
+                rhs=picked_words[c0 // HALF][:, c0 % HALF : c0 % HALF + c1 - c0].bitcast(FP8X4),
                 rhs_scale=planes[part][:, in_part : in_part + c1 - c0],
                 start=True,
                 stop=True,

@@ -68,7 +68,7 @@ def tile_picked_sub_lin_relu2_sub_p_kernel(tc, x_words, x_scales, w, b, gate, of
 
         nc.scalar.dma_start(scale_store[ROW0:P, :], x_scales[0].bitcast(I32))
         nc.sync.dma_start(offs_sb[:], offs)
-        nc.gpsimd.dma_start(bias[:], b)
+        nc.scalar.dma_start(bias[:], b)
         nc.sync.dma_start(word_store[:], x_words[0].rearrange("p c r -> p (c r)").bitcast(I32))
         nc.sync.dma_start(w_raw[:], w.rearrange("(p j) n -> p j n", j=PACK))
         nc.sync.dma_start(pos_sb[0][:], pos1)

@@ -50,6 +50,7 @@ def tile_picked_sub_lin_relu2_sub_p_kernel(tc, x_words, x_scales, w, b, gate, of
         w_codes = keep.tile([P, N], U32, name="w_codes", align_bytes=64)
         w_scales = keep.tile([P, N], U8, name="w_scales", align_bytes=64)
         bias = keep.tile([P, 1], F32, name="bias")
+        bias_row = keep.tile([P, N], F32, name="bias_row")
         picked_rows = [keep.tile([P, c1 - c0], U8, name="picked_rows%d" % h, align_bytes=64) for h, (c0, c1) in enumerate(SCALE_PARTS)]
         planes = [keep.tile([P, c1 - c0], U8, name="planes%d" % h, align_bytes=64) for h, (c0, c1) in enumerate(SCALE_PARTS)]
         rect = keep.tile([P, S], F32, name="rect")
@@ -65,15 +66,20 @@ def tile_picked_sub_lin_relu2_sub_p_kernel(tc, x_words, x_scales, w, b, gate, of
             nc.vector.memset(plane[:].bitcast(I32), 0)
 
         make_identity(nc, ident[:])
+        nc.gpsimd.memset(bias_row[0 : P - 1, :], 0.0)
 
         nc.scalar.dma_start(scale_store[ROW0:P, :], x_scales[0].bitcast(I32))
         nc.sync.dma_start(offs_sb[:], offs)
-        nc.scalar.dma_start(bias[:], b)
+        nc.scalar.dma_start(bias_row[P - 1 : P, :], b.rearrange("n o -> o n"))
         nc.sync.dma_start(word_store[:], x_words[0].rearrange("p c r -> p (c r)").bitcast(I32))
         nc.sync.dma_start(w_raw[:], w.rearrange("(p j) n -> p j n", j=PACK))
         nc.sync.dma_start(pos_sb[0][:], pos1)
         nc.sync.dma_start(pos_sb[1][:], pos2)
         nc.sync.dma_start(pos_sb[2][:], pos3)
+
+        bias_turned = psum.tile([P, P], F32, name="bias_turned", tag="bias_bank")
+        nc.tensor.transpose(bias_turned[:], bias_row[:], ident[:])
+        nc.scalar.copy(bias[:], bias_turned[:, P - 1 : P])
 
         for h, (c0, c1) in enumerate(SCALE_PARTS):
             nc.vector.tensor_copy(

@@ -136,7 +136,8 @@ def tile_picked_sub_lin_relu2_sub_p_kernel(tc, x_words, x_scales, w, b, gate, of
         for d in range(D):
             nc.vector.tensor_tensor(terms[:, d, :], y[:].indirect(pos_sb[d][:]), gate_sb[:, d, :], ALU.mult)
 
-        target_blocks = [slice(j * P, (j + 1) * P) for j in range(V // P)]
+        all_blocks = [slice(j * P, (j + 1) * P) for j in range(V // P)]
+        own_blocks, target_blocks = all_blocks[:-TURNED_BLOCKS], all_blocks[-TURNED_BLOCKS:]
         sums_t = [psum.tile([P, P], F32, name="sum_t%d" % j, tag="bank%d" % j) for j in range(TURNED_BLOCKS)]
         for d in range(2):
             for j in range(TURNED_BLOCKS):
@@ -150,13 +151,10 @@ def tile_picked_sub_lin_relu2_sub_p_kernel(tc, x_words, x_scales, w, b, gate, of
             nc.tensor.transpose(pair[:], turned[j][:], ident[:])
             bank_pairs.append(pair)
 
-        own_blocks = target_blocks[TURNED_BLOCKS:]
         for pair, cols in zip(own_pairs, own_blocks):
             nc.vector.tensor_tensor(pair[:], terms[:, 0, cols], terms[:, 1, cols], ALU.add)
-        for pair, cols in zip(own_pairs, own_blocks):
+        stores = {0: all_blocks[0], 2: slice(P, 3 * P), 3: all_blocks[3]}
+        for j, (pair, cols) in enumerate(zip(own_pairs + bank_pairs, all_blocks)):
             nc.vector.tensor_tensor(total[:, cols], pair[:], terms[:, 2, cols], ALU.add)
-        own_cols = slice(TURNED_BLOCKS * P, V)
-        nc.sync.dma_start(out[:, own_cols], total[:, own_cols])
-        for pair, cols in zip(bank_pairs, target_blocks):
-            nc.vector.tensor_tensor(total[:, cols], pair[:], terms[:, 2, cols], ALU.add)
-            nc.sync.dma_start(out[:, cols], total[:, cols])
+            if j in stores:
+                nc.sync.dma_start(out[:, stores[j]], total[:, stores[j]])

@@ -97,7 +97,12 @@ def tile_picked_sub_lin_relu2_sub_p_kernel(tc, x_words, x_scales, w, b, gate, of
             nc.sync.dma_start(gate_sb[:, d, :], gate[d])
 
         nc.scalar.activation(
-            w_bf[:].rearrange("p (c i) j -> p c j i", i=PACK), w_raw[:].rearrange("p j (c i) -> p c j i", i=PACK), ACT.Copy
+            w_bf[:, 0:80, :].rearrange("p (c i) j -> p c j i", i=PACK),
+            w_raw[:, :, 0:80].rearrange("p j (c i) -> p c j i", i=PACK),
+            ACT.Copy,
+        )
+        nc.gpsimd.tensor_scalar(
+            w_bf[:, 80:N, :], w_raw[:, :, 80:N].rearrange("p j n -> p n j"), 1.0, 0.0, ALU.mult, ALU.add
         )
         nc.vector.quantize_mx(w_codes[:].bitcast(FP8X4), w_scales[:], w_bf[:].rearrange("p n j -> p (n j)"))
 

@@ -61,12 +61,13 @@ def tile_picked_sub_lin_relu2_sub_p_kernel(tc, x_words, x_scales, w, b, gate, of
         own_pairs = [keep.tile([P, P], F32, name="own_pair%d" % j) for j in range(V // P - TURNED_BLOCKS)]
         total = keep.tile([P, V], F32, name="total")
 
+        nc.vector.memset(ident[:], 0.0)
         nc.vector.memset(scale_store[0:ROW0, :], 0)
         for plane in planes:
             nc.vector.memset(plane[:].bitcast(I32), 0)
+        nc.vector.memset(bias_row[0 : P - 1, :], 0.0)
 
-        make_identity(nc, ident[:])
-        nc.gpsimd.memset(bias_row[0 : P - 1, :], 0.0)
+        make_identity(nc, ident[:], nomemset=True)
 
         nc.scalar.dma_start(scale_store[ROW0:P, :], x_scales[0].bitcast(I32))
         nc.sync.dma_start(offs_sb[:], offs)

@@ -28,7 +28,7 @@ SCALE_PARTS = ((0, 640), (640, S))
 
 WORD_GATHERS = ((0, 512), (512, 768), (768, 1024))
 PIECES = ((0, 256), (256, 512), (512, 640), (640, 768), (768, 896), (896, 1024))
-TURNED_BLOCKS = 2
+BLOCKS = V // P
 
 
 def entries(list_tile, c0, c1):
@@ -51,14 +51,16 @@ def tile_picked_sub_lin_relu2_sub_p_kernel(tc, x_words, x_scales, w, b, gate, of
         w_scales = keep.tile([P, N], U8, name="w_scales", align_bytes=64)
         bias = keep.tile([P, 1], F32, name="bias")
         bias_row = keep.tile([P, N], F32, name="bias_row")
+        columns = keep.tile([P, BLOCKS], F32, name="columns")
         picked_rows = [keep.tile([P, c1 - c0], U8, name="picked_rows%d" % h, align_bytes=64) for h, (c0, c1) in enumerate(SCALE_PARTS)]
         planes = [keep.tile([P, c1 - c0], U8, name="planes%d" % h, align_bytes=64) for h, (c0, c1) in enumerate(SCALE_PARTS)]
         rect = keep.tile([P, S], F32, name="rect")
         y = keep.tile([P, S], F32, name="y")
-        terms = keep.tile([P, D, V], F32, name="terms")
+        terms = keep.tile([P, 2, V], F32, name="terms")
+        fetched = keep.tile([P, V], F32, name="fetched")
+        partial = keep.tile([P, V], F32, name="partial")
         ident = keep.tile([P, P], F32, name="ident")
-        turned = [keep.tile([P, P], F32, name="turned%d" % j) for j in range(TURNED_BLOCKS)]
-        own_pairs = [keep.tile([P, P], F32, name="own_pair%d" % j) for j in range(V // P - TURNED_BLOCKS)]
+        turned = [keep.tile([P, P], F32, name="turned%d" % j) for j in range(BLOCKS)]
         total = keep.tile([P, V], F32, name="total")
 
         nc.vector.memset(ident[:], 0.0)
@@ -78,7 +80,7 @@ def tile_picked_sub_lin_relu2_sub_p_kernel(tc, x_words, x_scales, w, b, gate, of
         nc.sync.dma_start(pos_sb[1][:], pos2)
         nc.sync.dma_start(pos_sb[2][:], pos3)
 
-        bias_turned = psum.tile([P, P], F32, name="bias_turned", tag="bias_bank")
+        bias_turned = psum.tile([P, P], F32, name="bias_turned", tag="bank6")
         nc.tensor.transpose(bias_turned[:], bias_row[:], ident[:])
         nc.scalar.copy(bias[:], bias_turned[:, P - 1 : P])
 
@@ -93,9 +95,12 @@ def tile_picked_sub_lin_relu2_sub_p_kernel(tc, x_words, x_scales, w, b, gate, of
                     picked_rows[h][ROW0 + r : P : ROWS_PER_QUADRANT, :].bitcast(I32),
                 )
 
-        gate_sb = keep.tile([P, D, V], F32, name="gate_sb", tag="scale_then_gate", align_bytes=64)
-        for d in range(D):
-            nc.sync.dma_start(gate_sb[:, d, :], gate[d])
+        gate_all = keep.tile([P, 2 * V + P], F32, name="gate_all", tag="scale_then_gate", align_bytes=64)
+        gate_rows = gate_all[:, 0:P]
+        gate_sb = [gate_all[:, P + d * V : P + (d + 1) * V] for d in range(2)]
+        nc.sync.dma_start(gate_rows, gate[2, 0 : P // BLOCKS, :].rearrange("m (j v) -> (m j) v", v=P))
+        for d in range(2):
+            nc.sync.dma_start(gate_sb[d], gate[d])
 
         nc.scalar.activation(
             w_bf[:, 0:80, :].rearrange("p (c i) j -> p c j i", i=PACK),
@@ -133,34 +138,37 @@ def tile_picked_sub_lin_relu2_sub_p_kernel(tc, x_words, x_scales, w, b, gate, of
                 stop=True,
             )
 
+        gate_turned = psum.tile([P, P], F32, name="gate_turned", tag="bank6")
+        nc.tensor.transpose(gate_turned[:], gate_rows, ident[:])
+        nc.vector.tensor_copy(columns[:], gate_turned[:, 0:BLOCKS])
+
         piece_cols = [slice(c0, c1) for c0, c1 in PIECES]
         for i, cols in enumerate(piece_cols):
             nc.scalar.activation(rect[:, cols], accs[i][:], ACT.Relu, bias=bias[:])
         for cols in piece_cols:
             nc.vector.tensor_tensor(y[:, cols], rect[:, cols], rect[:, cols], ALU.mult)
 
-        for d in range(D):
-            nc.vector.tensor_tensor(terms[:, d, :], y[:].indirect(pos_sb[d][:]), gate_sb[:, d, :], ALU.mult)
+        blocks = [slice(j * P, (j + 1) * P) for j in range(BLOCKS)]
+        halves = [slice(h * V // 2, (h + 1) * V // 2) for h in range(2)]
+        nc.vector.tensor_tensor(terms[:, 0, :], y[:].indirect(pos_sb[0][:]), gate_sb[0], ALU.mult)
+        for cols in halves:
+            nc.vector.tensor_tensor(
+                terms[:, 1, cols], y[:].indirect(entries(pos_sb[1], cols.start, cols.stop)), gate_sb[1][:, cols], ALU.mult
+            )
 
-        all_blocks = [slice(j * P, (j + 1) * P) for j in range(V // P)]
-        own_blocks, target_blocks = all_blocks[:-TURNED_BLOCKS], all_blocks[-TURNED_BLOCKS:]
-        sums_t = [psum.tile([P, P], F32, name="sum_t%d" % j, tag="bank%d" % j) for j in range(TURNED_BLOCKS)]
-        for d in range(2):
-            for j in range(TURNED_BLOCKS):
-                nc.tensor.matmul(
-                    sums_t[j][:], terms[:, d, target_blocks[j]], ident[:], start=(d == 0), stop=(d == 1), is_transpose=True
-                )
-        bank_pairs = []
-        for j in range(TURNED_BLOCKS):
-            nc.scalar.copy(turned[j][:], sums_t[j][:])
-            pair = psum.tile([P, P], F32, name="pair%d" % j, tag="bank%d" % (TURNED_BLOCKS + j))
-            nc.tensor.transpose(pair[:], turned[j][:], ident[:])
-            bank_pairs.append(pair)
+        forth = [psum.tile([P, P], F32, name="forth%d" % j, tag="bank%d" % j) for j in range(BLOCKS)]
+        for j, cols in enumerate(blocks):
+            nc.scalar.activation(fetched[:, cols], y[:].indirect(entries(pos_sb[2], cols.start, cols.stop)), ACT.Copy)
+            nc.tensor.transpose(forth[j][:], fetched[:, cols], ident[:])
+        back = [psum.tile([P, P], F32, name="back%d" % j, tag="bank%d" % (BLOCKS + j)) for j in range(BLOCKS)]
+        for j in range(BLOCKS):
+            nc.scalar.activation(turned[j][:], forth[j][:], ACT.Copy, scale=columns[:, j : j + 1])
+            nc.tensor.transpose(back[j][:], turned[j][:], ident[:])
 
-        for pair, cols in zip(own_pairs, own_blocks):
-            nc.vector.tensor_tensor(pair[:], terms[:, 0, cols], terms[:, 1, cols], ALU.add)
-        stores = {0: all_blocks[0], 2: slice(P, 3 * P), 3: all_blocks[3]}
-        for j, (pair, cols) in enumerate(zip(own_pairs + bank_pairs, all_blocks)):
-            nc.vector.tensor_tensor(total[:, cols], pair[:], terms[:, 2, cols], ALU.add)
+        for cols in halves:
+            nc.vector.tensor_tensor(partial[:, cols], terms[:, 0, cols], terms[:, 1, cols], ALU.add)
+        stores = {0: blocks[0], 2: slice(P, 3 * P), 3: blocks[3]}
+        for j, cols in enumerate(blocks):
+            nc.vector.tensor_tensor(total[:, cols], back[j][:], partial[:, cols], ALU.add)
             if j in stores:
                 nc.sync.dma_start(out[:, stores[j]], total[:, stores[j]])

@@ -51,16 +51,16 @@ def tile_picked_sub_lin_relu2_sub_p_kernel(tc, x_words, x_scales, w, b, gate, of
         w_scales = keep.tile([P, N], U8, name="w_scales", align_bytes=64)
         bias = keep.tile([P, 1], F32, name="bias")
         bias_row = keep.tile([P, N], F32, name="bias_row")
-        columns = keep.tile([P, BLOCKS], F32, name="columns")
+        columns = keep.tile([P, 2 * BLOCKS], F32, name="columns")
         picked_rows = [keep.tile([P, c1 - c0], U8, name="picked_rows%d" % h, align_bytes=64) for h, (c0, c1) in enumerate(SCALE_PARTS)]
         planes = [keep.tile([P, c1 - c0], U8, name="planes%d" % h, align_bytes=64) for h, (c0, c1) in enumerate(SCALE_PARTS)]
         rect = keep.tile([P, S], F32, name="rect")
         y = keep.tile([P, S], F32, name="y")
         terms = keep.tile([P, 2, V], F32, name="terms")
-        fetched = keep.tile([P, V], F32, name="fetched")
+        fetched = keep.tile([P, 2, V], F32, name="fetched")
         partial = keep.tile([P, V], F32, name="partial")
         ident = keep.tile([P, P], F32, name="ident")
-        turned = [keep.tile([P, P], F32, name="turned%d" % j) for j in range(BLOCKS)]
+        turned = [keep.tile([P, P], F32, name="turned%d" % j) for j in range(BLOCKS + 1)]
         total = keep.tile([P, V], F32, name="total")
 
         nc.vector.memset(ident[:], 0.0)
@@ -98,9 +98,10 @@ def tile_picked_sub_lin_relu2_sub_p_kernel(tc, x_words, x_scales, w, b, gate, of
         gate_all = keep.tile([P, 2 * V + P], F32, name="gate_all", tag="scale_then_gate", align_bytes=64)
         gate_rows = gate_all[:, 0:P]
         gate_sb = [gate_all[:, P + d * V : P + (d + 1) * V] for d in range(2)]
-        nc.sync.dma_start(gate_rows, gate[2, 0 : P // BLOCKS, :].rearrange("m (j v) -> (m j) v", v=P))
-        for d in range(2):
-            nc.sync.dma_start(gate_sb[d], gate[d])
+        seam = gate.rearrange("d m (j v) -> (d m j) v", v=P)[2 * N * BLOCKS - P // 2 : 2 * N * BLOCKS + P // 2, :]
+        nc.sync.dma_start(gate_rows, seam)
+        nc.sync.dma_start(gate_sb[1][:, P:V], gate[1][:, P:V])
+        nc.sync.dma_start(gate_sb[0], gate[0])
 
         nc.scalar.activation(
             w_bf[:, 0:80, :].rearrange("p (c i) j -> p c j i", i=PACK),
@@ -140,7 +141,7 @@ def tile_picked_sub_lin_relu2_sub_p_kernel(tc, x_words, x_scales, w, b, gate, of
 
         gate_turned = psum.tile([P, P], F32, name="gate_turned", tag="bank6")
         nc.tensor.transpose(gate_turned[:], gate_rows, ident[:])
-        nc.vector.tensor_copy(columns[:], gate_turned[:, 0:BLOCKS])
+        nc.vector.tensor_copy(columns[:], gate_turned[:, P // 2 - BLOCKS : P // 2 + BLOCKS])
 
         piece_cols = [slice(c0, c1) for c0, c1 in PIECES]
         for i, cols in enumerate(piece_cols):
@@ -149,26 +150,28 @@ def tile_picked_sub_lin_relu2_sub_p_kernel(tc, x_words, x_scales, w, b, gate, of
             nc.vector.tensor_tensor(y[:, cols], rect[:, cols], rect[:, cols], ALU.mult)
 
         blocks = [slice(j * P, (j + 1) * P) for j in range(BLOCKS)]
-        halves = [slice(h * V // 2, (h + 1) * V // 2) for h in range(2)]
-        nc.vector.tensor_tensor(terms[:, 0, :], y[:].indirect(pos_sb[0][:]), gate_sb[0], ALU.mult)
-        for cols in halves:
+        rest = slice(P, V)
+        for d, cols in ((1, rest), (0, rest), (0, blocks[0])):
             nc.vector.tensor_tensor(
-                terms[:, 1, cols], y[:].indirect(entries(pos_sb[1], cols.start, cols.stop)), gate_sb[1][:, cols], ALU.mult
+                terms[:, d, cols], y[:].indirect(entries(pos_sb[d], cols.start, cols.stop)), gate_sb[d][:, cols], ALU.mult
             )
 
-        forth = [psum.tile([P, P], F32, name="forth%d" % j, tag="bank%d" % j) for j in range(BLOCKS)]
-        for j, cols in enumerate(blocks):
-            nc.scalar.activation(fetched[:, cols], y[:].indirect(entries(pos_sb[2], cols.start, cols.stop)), ACT.Copy)
-            nc.tensor.transpose(forth[j][:], fetched[:, cols], ident[:])
-        back = [psum.tile([P, P], F32, name="back%d" % j, tag="bank%d" % (BLOCKS + j)) for j in range(BLOCKS)]
-        for j in range(BLOCKS):
-            nc.scalar.activation(turned[j][:], forth[j][:], ACT.Copy, scale=columns[:, j : j + 1])
-            nc.tensor.transpose(back[j][:], turned[j][:], ident[:])
+        for d, cols in ((1, blocks[0]), (2, slice(0, V // 2)), (2, slice(V // 2, V))):
+            nc.scalar.activation(fetched[:, d - 1, cols], y[:].indirect(entries(pos_sb[d], cols.start, cols.stop)), ACT.Copy)
+        turns = [(1, 0)] + [(2, j) for j in range(BLOCKS)]
+        forth = [psum.tile([P, P], F32, name="forth%d" % i, tag="bank%d" % i) for i in range(len(turns))]
+        for bank, (d, j) in zip(forth, turns):
+            nc.tensor.transpose(bank[:], fetched[:, d - 1, blocks[j]], ident[:])
+        back = [psum.tile([P, P], F32, name="back%d" % j, tag="bank%d" % ((len(turns) + j) % 8)) for j in range(BLOCKS)]
+        for i, (d, j) in enumerate(turns):
+            column = (d - 1) * BLOCKS + j
+            nc.scalar.activation(turned[i][:], forth[i][:], ACT.Copy, scale=columns[:, column : column + 1])
+            nc.tensor.matmul(back[j][:], turned[i][:], ident[:], start=(d == 1 or j > 0), stop=(d == 2), is_transpose=True)
 
-        for cols in halves:
-            nc.vector.tensor_tensor(partial[:, cols], terms[:, 0, cols], terms[:, 1, cols], ALU.add)
+        nc.vector.tensor_tensor(partial[:, rest], terms[:, 0, rest], terms[:, 1, rest], ALU.add)
         stores = {0: blocks[0], 2: slice(P, 3 * P), 3: blocks[3]}
         for j, cols in enumerate(blocks):
-            nc.vector.tensor_tensor(total[:, cols], back[j][:], partial[:, cols], ALU.add)
+            own = terms[:, 0, cols] if j == 0 else partial[:, cols]
+            nc.vector.tensor_tensor(total[:, cols], back[j][:], own, ALU.add)
             if j in stores:
                 nc.sync.dma_start(out[:, stores[j]], total[:, stores[j]])

@@ -56,11 +56,10 @@ def tile_picked_sub_lin_relu2_sub_p_kernel(tc, x_words, x_scales, w, b, gate, of
         planes = [keep.tile([P, c1 - c0], U8, name="planes%d" % h, align_bytes=64) for h, (c0, c1) in enumerate(SCALE_PARTS)]
         rect = keep.tile([P, S], F32, name="rect")
         y = keep.tile([P, S], F32, name="y")
-        terms = keep.tile([P, 2, V], F32, name="terms")
-        fetched = keep.tile([P, 2, V], F32, name="fetched")
-        partial = keep.tile([P, V], F32, name="partial")
+        terms = keep.tile([P, D, V], F32, name="terms")
+        partial = keep.tile([P, V // 2], F32, name="partial")
         ident = keep.tile([P, P], F32, name="ident")
-        turned = [keep.tile([P, P], F32, name="turned%d" % j) for j in range(BLOCKS + 1)]
+        turned = [keep.tile([P, P], F32, name="turned%d" % j) for j in range(BLOCKS)]
         total = keep.tile([P, V], F32, name="total")
 
         nc.vector.memset(ident[:], 0.0)
@@ -97,10 +96,12 @@ def tile_picked_sub_lin_relu2_sub_p_kernel(tc, x_words, x_scales, w, b, gate, of
 
         gate_all = keep.tile([P, 2 * V + P], F32, name="gate_all", tag="scale_then_gate", align_bytes=64)
         gate_rows = gate_all[:, 0:P]
-        gate_sb = [gate_all[:, P + d * V : P + (d + 1) * V] for d in range(2)]
+        gate_sb = [gate_all[:, P : P + V], gate_all[:, P + V : P + V + V // 2], gate_all[:, P + V + V // 2 : P + 2 * V]]
         seam = gate.rearrange("d m (j v) -> (d m j) v", v=P)[2 * N * BLOCKS - P // 2 : 2 * N * BLOCKS + P // 2, :]
         nc.sync.dma_start(gate_rows, seam)
-        nc.sync.dma_start(gate_sb[1][:, P:V], gate[1][:, P:V])
+        nc.sync.dma_start(
+            gate_all[:, P + V : P + 2 * V].rearrange("m (d v) -> m d v", d=2), gate[1:D, :, 0 : V // 2].rearrange("d m v -> m d v")
+        )
         nc.sync.dma_start(gate_sb[0], gate[0])
 
         nc.scalar.activation(
@@ -150,28 +151,31 @@ def tile_picked_sub_lin_relu2_sub_p_kernel(tc, x_words, x_scales, w, b, gate, of
             nc.vector.tensor_tensor(y[:, cols], rect[:, cols], rect[:, cols], ALU.mult)
 
         blocks = [slice(j * P, (j + 1) * P) for j in range(BLOCKS)]
-        rest = slice(P, V)
-        for d, cols in ((1, rest), (0, rest), (0, blocks[0])):
+        front, rear = slice(0, V // 2), slice(V // 2, V)
+        for d, cols in ((1, rear), (2, blocks[2]), (2, blocks[3])):
+            nc.scalar.activation(terms[:, d, cols], y[:].indirect(entries(pos_sb[d], cols.start, cols.stop)), ACT.Copy)
+        turns = [(d, j) for d in (1, 2) for j in (2, 3)]
+        forth = [psum.tile([P, P], F32, name="forth%d" % i, tag="bank%d" % i) for i in range(len(turns))]
+        for bank, (d, j) in zip(forth, turns):
+            nc.tensor.transpose(bank[:], terms[:, d, blocks[j]], ident[:])
+        back = {j: psum.tile([P, P], F32, name="back%d" % j, tag="bank%d" % (2 + j)) for j in (2, 3)}
+        for i, (d, j) in enumerate(turns):
+            column = (d - 1) * BLOCKS + j
+            nc.scalar.activation(turned[i][:], forth[i][:], ACT.Copy, scale=columns[:, column : column + 1])
+            nc.tensor.matmul(back[j][:], turned[i][:], ident[:], start=(d == 1), stop=(d == 2), is_transpose=True)
+
+        def fetch(d, cols):
             nc.vector.tensor_tensor(
                 terms[:, d, cols], y[:].indirect(entries(pos_sb[d], cols.start, cols.stop)), gate_sb[d][:, cols], ALU.mult
             )
 
-        for d, cols in ((1, blocks[0]), (2, slice(0, V // 2)), (2, slice(V // 2, V))):
-            nc.scalar.activation(fetched[:, d - 1, cols], y[:].indirect(entries(pos_sb[d], cols.start, cols.stop)), ACT.Copy)
-        turns = [(1, 0)] + [(2, j) for j in range(BLOCKS)]
-        forth = [psum.tile([P, P], F32, name="forth%d" % i, tag="bank%d" % i) for i in range(len(turns))]
-        for bank, (d, j) in zip(forth, turns):
-            nc.tensor.transpose(bank[:], fetched[:, d - 1, blocks[j]], ident[:])
-        back = [psum.tile([P, P], F32, name="back%d" % j, tag="bank%d" % ((len(turns) + j) % 8)) for j in range(BLOCKS)]
-        for i, (d, j) in enumerate(turns):
-            column = (d - 1) * BLOCKS + j
-            nc.scalar.activation(turned[i][:], forth[i][:], ACT.Copy, scale=columns[:, column : column + 1])
-            nc.tensor.matmul(back[j][:], turned[i][:], ident[:], start=(d == 1 or j > 0), stop=(d == 2), is_transpose=True)
-
-        nc.vector.tensor_tensor(partial[:, rest], terms[:, 0, rest], terms[:, 1, rest], ALU.add)
-        stores = {0: blocks[0], 2: slice(P, 3 * P), 3: blocks[3]}
-        for j, cols in enumerate(blocks):
-            own = terms[:, 0, cols] if j == 0 else partial[:, cols]
-            nc.vector.tensor_tensor(total[:, cols], back[j][:], own, ALU.add)
-            if j in stores:
-                nc.sync.dma_start(out[:, stores[j]], total[:, stores[j]])
+        fetch(1, front)
+        fetch(2, front)
+        fetch(0, front)
+        nc.vector.tensor_tensor(partial[:], terms[:, 1, front], terms[:, 2, front], ALU.add)
+        fetch(0, rear)
+        nc.vector.tensor_tensor(total[:, front], partial[:], terms[:, 0, front], ALU.add)
+        nc.sync.dma_start(out[:, front], total[:, front])
+        for j in (2, 3):
+            nc.vector.tensor_tensor(total[:, blocks[j]], back[j][:], terms[:, 0, blocks[j]], ALU.add)
+            nc.sync.dma_start(out[:, blocks[j]], total[:, blocks[j]])

@@ -26,8 +26,8 @@ SCALE_ROWS = K // 32
 ROW0 = P - SCALE_ROWS
 SCALE_PARTS = ((0, 640), (640, S))
 
-WORD_GATHERS = ((0, 512), (512, 768), (768, 1024))
-PIECES = ((0, 256), (256, 512), (512, 640), (640, 768), (768, 896), (896, 1024))
+WORD_GATHERS = ((0, 512), (512, 768), (768, 896), (896, 1024))
+PIECES = tuple((c, c + 128) for c in range(0, S, 128))
 BLOCKS = V // P
 
 
@@ -79,7 +79,7 @@ def tile_picked_sub_lin_relu2_sub_p_kernel(tc, x_words, x_scales, w, b, gate, of
         nc.sync.dma_start(pos_sb[1][:], pos2)
         nc.sync.dma_start(pos_sb[2][:], pos3)
 
-        bias_turned = psum.tile([P, P], F32, name="bias_turned", tag="bank6")
+        bias_turned = psum.tile([P, P], F32, name="bias_turned", tag="bank7")
         nc.tensor.transpose(bias_turned[:], bias_row[:], ident[:])
         nc.scalar.copy(bias[:], bias_turned[:, P - 1 : P])
 
@@ -140,15 +140,15 @@ def tile_picked_sub_lin_relu2_sub_p_kernel(tc, x_words, x_scales, w, b, gate, of
                 stop=True,
             )
 
-        gate_turned = psum.tile([P, P], F32, name="gate_turned", tag="bank6")
-        nc.tensor.transpose(gate_turned[:], gate_rows, ident[:])
-        nc.vector.tensor_copy(columns[:], gate_turned[:, P // 2 - BLOCKS : P // 2 + BLOCKS])
-
         piece_cols = [slice(c0, c1) for c0, c1 in PIECES]
         for i, cols in enumerate(piece_cols):
             nc.scalar.activation(rect[:, cols], accs[i][:], ACT.Relu, bias=bias[:])
         for cols in piece_cols:
             nc.vector.tensor_tensor(y[:, cols], rect[:, cols], rect[:, cols], ALU.mult)
+
+        gate_turned = psum.tile([P, P], F32, name="gate_turned", tag="bank4")
+        nc.tensor.transpose(gate_turned[:], gate_rows, ident[:])
+        nc.scalar.copy(columns[:], gate_turned[:, P // 2 - BLOCKS : P // 2 + BLOCKS])
 
         blocks = [slice(j * P, (j + 1) * P) for j in range(BLOCKS)]
         front, rear = slice(0, V // 2), slice(V // 2, V)

@@ -51,7 +51,6 @@ def tile_picked_sub_lin_relu2_sub_p_kernel(tc, x_words, x_scales, w, b, gate, of
         w_scales = keep.tile([P, N], U8, name="w_scales", align_bytes=64)
         bias = keep.tile([P, 1], F32, name="bias")
         bias_row = keep.tile([P, N], F32, name="bias_row")
-        columns = keep.tile([P, 2 * BLOCKS], F32, name="columns")
         picked_rows = [keep.tile([P, c1 - c0], U8, name="picked_rows%d" % h, align_bytes=64) for h, (c0, c1) in enumerate(SCALE_PARTS)]
         planes = [keep.tile([P, c1 - c0], U8, name="planes%d" % h, align_bytes=64) for h, (c0, c1) in enumerate(SCALE_PARTS)]
         rect = keep.tile([P, S], F32, name="rect")
@@ -94,15 +93,15 @@ def tile_picked_sub_lin_relu2_sub_p_kernel(tc, x_words, x_scales, w, b, gate, of
                     picked_rows[h][ROW0 + r : P : ROWS_PER_QUADRANT, :].bitcast(I32),
                 )
 
-        gate_all = keep.tile([P, 2 * V + P], F32, name="gate_all", tag="scale_then_gate", align_bytes=64)
-        gate_rows = gate_all[:, 0:P]
-        gate_sb = [gate_all[:, P : P + V], gate_all[:, P + V : P + V + V // 2], gate_all[:, P + V + V // 2 : P + 2 * V]]
-        seam = gate.rearrange("d m (j v) -> (d m j) v", v=P)[2 * N * BLOCKS - P // 2 : 2 * N * BLOCKS + P // 2, :]
-        nc.sync.dma_start(gate_rows, seam)
-        nc.sync.dma_start(
-            gate_all[:, P + V : P + 2 * V].rearrange("m (d v) -> m d v", d=2), gate[1:D, :, 0 : V // 2].rearrange("d m v -> m d v")
-        )
-        nc.sync.dma_start(gate_sb[0], gate[0])
+        gate_all = keep.tile([P, 2 * V + 16], F32, name="gate_all", tag="scale_then_gate", align_bytes=64)
+        gate_front = gate_all[:, 0 : D * V // 2].rearrange("m (d v) -> m d v", d=D)
+        gate_rear = gate_all[:, D * V // 2 : 2 * V]
+        columns = gate_all[:, 2 * V : 2 * V + 16]
+        nc.sync.dma_start(gate_front, gate[:, :, 0 : V // 2].rearrange("d m v -> m d v"))
+        nc.sync.dma_start(gate_rear, gate[0, :, V // 2 : V])
+        with nc.allow_non_contiguous_dma(reason="one gate a partition"):
+            for d in (1, 2):
+                nc.sync.dma_start(columns[:, 8 * d - 8 : 8 * d - 6], gate[d, 0, V // 2 : V].rearrange("(j v) -> v j", v=P))
 
         nc.scalar.activation(
             w_bf[:, 0:80, :].rearrange("p (c i) j -> p c j i", i=PACK),
@@ -146,10 +145,6 @@ def tile_picked_sub_lin_relu2_sub_p_kernel(tc, x_words, x_scales, w, b, gate, of
         for cols in piece_cols:
             nc.vector.tensor_tensor(y[:, cols], rect[:, cols], rect[:, cols], ALU.mult)
 
-        gate_turned = psum.tile([P, P], F32, name="gate_turned", tag="bank4")
-        nc.tensor.transpose(gate_turned[:], gate_rows, ident[:])
-        nc.scalar.copy(columns[:], gate_turned[:, P // 2 - BLOCKS : P // 2 + BLOCKS])
-
         blocks = [slice(j * P, (j + 1) * P) for j in range(BLOCKS)]
         front, rear = slice(0, V // 2), slice(V // 2, V)
         for d, cols in ((1, rear), (2, blocks[2]), (2, blocks[3])):
@@ -160,14 +155,13 @@ def tile_picked_sub_lin_relu2_sub_p_kernel(tc, x_words, x_scales, w, b, gate, of
             nc.tensor.transpose(bank[:], terms[:, d, blocks[j]], ident[:])
         back = {j: psum.tile([P, P], F32, name="back%d" % j, tag="bank%d" % (2 + j)) for j in (2, 3)}
         for i, (d, j) in enumerate(turns):
-            column = (d - 1) * BLOCKS + j
+            column = (d - 1) * 8 + j - 2
             nc.scalar.activation(turned[i][:], forth[i][:], ACT.Copy, scale=columns[:, column : column + 1])
             nc.tensor.matmul(back[j][:], turned[i][:], ident[:], start=(d == 1), stop=(d == 2), is_transpose=True)
 
         def fetch(d, cols):
-            nc.vector.tensor_tensor(
-                terms[:, d, cols], y[:].indirect(entries(pos_sb[d], cols.start, cols.stop)), gate_sb[d][:, cols], ALU.mult
-            )
+            gates = gate_front[:, d, :] if cols == front else gate_rear
+            nc.vector.tensor_tensor(terms[:, d, cols], y[:].indirect(entries(pos_sb[d], cols.start, cols.stop)), gates, ALU.mult)
 
         fetch(1, front)
         fetch(2, front)

@@ -51,7 +51,7 @@ def tile_picked_sub_lin_relu2_sub_p_kernel(tc, x_words, x_scales, w, b, gate, of
         w_scales = keep.tile([P, N], U8, name="w_scales", align_bytes=64)
         bias = keep.tile([P, 1], F32, name="bias")
         bias_row = keep.tile([P, N], F32, name="bias_row")
-        picked_rows = [keep.tile([P, c1 - c0], U8, name="picked_rows%d" % h, align_bytes=64) for h, (c0, c1) in enumerate(SCALE_PARTS)]
+        picked_rows = [keep.tile([P, c1 - c0], U8, name="picked_rows%d" % h, tag="rows%d" % h, align_bytes=64) for h, (c0, c1) in enumerate(SCALE_PARTS)]
         planes = [keep.tile([P, c1 - c0], U8, name="planes%d" % h, align_bytes=64) for h, (c0, c1) in enumerate(SCALE_PARTS)]
         rect = keep.tile([P, S], F32, name="rect")
         y = keep.tile([P, S], F32, name="y")
@@ -93,10 +93,10 @@ def tile_picked_sub_lin_relu2_sub_p_kernel(tc, x_words, x_scales, w, b, gate, of
                     picked_rows[h][ROW0 + r : P : ROWS_PER_QUADRANT, :].bitcast(I32),
                 )
 
-        gate_all = keep.tile([P, 2 * V + 16], F32, name="gate_all", tag="scale_then_gate", align_bytes=64)
+        gate_all = keep.tile([P, 2 * V], F32, name="gate_all", tag="scale_then_gate", align_bytes=64)
         gate_front = gate_all[:, 0 : D * V // 2].rearrange("m (d v) -> m d v", d=D)
         gate_rear = gate_all[:, D * V // 2 : 2 * V]
-        columns = gate_all[:, 2 * V : 2 * V + 16]
+        columns = keep.tile([P, 16], F32, name="columns", tag="rows1", align_bytes=64)
         nc.sync.dma_start(gate_front, gate[:, :, 0 : V // 2].rearrange("d m v -> m d v"))
         nc.sync.dma_start(gate_rear, gate[0, :, V // 2 : V])
         with nc.allow_non_contiguous_dma(reason="one gate a partition"):

@@ -159,17 +159,20 @@ def tile_picked_sub_lin_relu2_sub_p_kernel(tc, x_words, x_scales, w, b, gate, of
             nc.scalar.activation(turned[i][:], forth[i][:], ACT.Copy, scale=columns[:, column : column + 1])
             nc.tensor.matmul(back[j][:], turned[i][:], ident[:], start=(d == 1), stop=(d == 2), is_transpose=True)
 
-        def fetch(d, cols):
-            gates = gate_front[:, d, :] if cols == front else gate_rear
-            nc.vector.tensor_tensor(terms[:, d, cols], y[:].indirect(entries(pos_sb[d], cols.start, cols.stop)), gates, ALU.mult)
+        def fetch(d, cols, gates, into):
+            nc.vector.tensor_tensor(into, y[:].indirect(entries(pos_sb[d], cols.start, cols.stop)), gates, ALU.mult)
 
-        fetch(1, front)
-        fetch(2, front)
-        fetch(0, front)
-        nc.vector.tensor_tensor(partial[:], terms[:, 1, front], terms[:, 2, front], ALU.add)
-        fetch(0, rear)
-        nc.vector.tensor_tensor(total[:, front], partial[:], terms[:, 0, front], ALU.add)
-        nc.sync.dma_start(out[:, front], total[:, front])
-        for j in (2, 3):
-            nc.vector.tensor_tensor(total[:, blocks[j]], back[j][:], terms[:, 0, blocks[j]], ALU.add)
+        def finish(j, first, second):
+            nc.vector.tensor_tensor(total[:, blocks[j]], first, second, ALU.add)
             nc.sync.dma_start(out[:, blocks[j]], total[:, blocks[j]])
+
+        for d in (1, 2, 0):
+            fetch(d, front, gate_front[:, d, :], terms[:, d, front])
+        nc.vector.tensor_tensor(partial[:], terms[:, 1, front], terms[:, 2, front], ALU.add)
+        own = {2: terms[:, 0, blocks[2]], 3: terms[:, 1, blocks[0]]}
+        fetch(0, blocks[2], gate_rear[:, 0:P], own[2])
+        finish(0, partial[:, blocks[0]], terms[:, 0, blocks[0]])
+        fetch(0, blocks[3], gate_rear[:, P : 2 * P], own[3])
+        finish(1, partial[:, blocks[1]], terms[:, 0, blocks[1]])
+        for j in (2, 3):
+            finish(j, back[j][:], own[j])

from contextlib import ExitStack

import concourse.mybir as mybir
from concourse.masks import make_identity

K, T, D, S, V, N = 512, 2048, 3, 1024, 512, 128
FLOPS = 2 * K * S * N

F32 = mybir.dt.float32
BF16 = mybir.dt.bfloat16
I32 = mybir.dt.int32
U32 = mybir.dt.uint32
U16 = mybir.dt.uint16
U8 = mybir.dt.uint8
FP8X4 = mybir.dt.float8_e4m3fn_x4
ACT = mybir.ActivationFunctionType
ALU = mybir.AluOpType

P = 128
PACK = 4
LANES = 16
QUADRANT = 32
ROWS_PER_QUADRANT = 4
HALF = S // 2
SCALE_ROWS = K // 32
ROW0 = P - SCALE_ROWS
SCALE_PARTS = ((0, 640), (640, S))

WORD_GATHERS = ((0, 512), (512, 768), (768, 896), (896, 1024))
PIECES = tuple((c, c + 128) for c in range(0, S, 128))
BLOCKS = V // P


def entries(list_tile, c0, c1):
    return list_tile[:, c0 // LANES : c1 // LANES]


def tile_picked_sub_lin_relu2_sub_p_kernel(tc, x_words, x_scales, w, b, gate, offs, pos1, pos2, pos3, out):
    nc = tc.nc
    with ExitStack() as ctx:
        keep = ctx.enter_context(tc.tile_pool(name="keep", bufs=1))
        psum = ctx.enter_context(tc.psum_pool(name="psum", bufs=1))

        offs_sb = keep.tile([P, S // LANES], U16, name="offs_sb")
        pos_sb = [keep.tile([P, V // LANES], U16, name="pos_sb%d" % d) for d in range(D)]
        scale_store = keep.tile([P, T // 4], I32, name="scale_store", tag="scale_then_gate", align_bytes=64)
        word_store = keep.tile([P, T], I32, name="word_store", align_bytes=64)
        w_raw = keep.tile([P, PACK, N], F32, name="w_raw", tag="w_then_words", align_bytes=64)
        w_bf = keep.tile([P, N, PACK], BF16, name="w_bf", align_bytes=64)
        w_codes = keep.tile([P, N], U32, name="w_codes", align_bytes=64)
        w_scales = keep.tile([P, N], U8, name="w_scales", align_bytes=64)
        bias = keep.tile([P, 1], F32, name="bias")
        bias_row = keep.tile([P, N], F32, name="bias_row")
        picked_rows = [keep.tile([P, c1 - c0], U8, name="picked_rows%d" % h, tag="rows%d" % h, align_bytes=64) for h, (c0, c1) in enumerate(SCALE_PARTS)]
        planes = [keep.tile([P, c1 - c0], U8, name="planes%d" % h, align_bytes=64) for h, (c0, c1) in enumerate(SCALE_PARTS)]
        rect = keep.tile([P, S], F32, name="rect")
        y = keep.tile([P, S], F32, name="y")
        terms = keep.tile([P, D, V], F32, name="terms")
        partial = keep.tile([P, V // 2], F32, name="partial")
        ident = keep.tile([P, P], F32, name="ident")
        turned = [keep.tile([P, P], F32, name="turned%d" % j) for j in range(BLOCKS)]
        total = keep.tile([P, V], F32, name="total")

        nc.vector.memset(ident[:], 0.0)
        nc.vector.memset(scale_store[0:ROW0, :], 0)
        for plane in planes:
            nc.vector.memset(plane[:].bitcast(I32), 0)
        nc.vector.memset(bias_row[0 : P - 1, :], 0.0)

        make_identity(nc, ident[:], nomemset=True)

        nc.scalar.dma_start(scale_store[ROW0:P, :], x_scales[0].bitcast(I32))
        nc.sync.dma_start(offs_sb[:], offs)
        nc.scalar.dma_start(bias_row[P - 1 : P, :], b.rearrange("n o -> o n"))
        nc.sync.dma_start(word_store[:], x_words[0].rearrange("p c r -> p (c r)").bitcast(I32))
        nc.sync.dma_start(w_raw[:], w.rearrange("(p j) n -> p j n", j=PACK))
        nc.sync.dma_start(pos_sb[0][:], pos1)
        nc.sync.dma_start(pos_sb[1][:], pos2)
        nc.sync.dma_start(pos_sb[2][:], pos3)

        bias_turned = psum.tile([P, P], F32, name="bias_turned", tag="bank7")
        nc.tensor.transpose(bias_turned[:], bias_row[:], ident[:])
        nc.scalar.copy(bias[:], bias_turned[:, P - 1 : P])

        for h, (c0, c1) in enumerate(SCALE_PARTS):
            nc.vector.tensor_copy(
                picked_rows[h][:],
                scale_store[:].bitcast(U8).indirect(entries(offs_sb, c0, c1)),
            )
            for r in range(ROWS_PER_QUADRANT):
                nc.sync.dma_start(
                    planes[h][r:P:QUADRANT, :].bitcast(I32),
                    picked_rows[h][ROW0 + r : P : ROWS_PER_QUADRANT, :].bitcast(I32),
                )

        gate_all = keep.tile([P, 2 * V], F32, name="gate_all", tag="scale_then_gate", align_bytes=64)
        gate_front = gate_all[:, 0 : D * V // 2].rearrange("m (d v) -> m d v", d=D)
        gate_rear = gate_all[:, D * V // 2 : 2 * V]
        columns = keep.tile([P, 16], F32, name="columns", tag="rows1", align_bytes=64)
        nc.sync.dma_start(gate_front, gate[:, :, 0 : V // 2].rearrange("d m v -> m d v"))
        nc.sync.dma_start(gate_rear, gate[0, :, V // 2 : V])
        with nc.allow_non_contiguous_dma(reason="one gate a partition"):
            for d in (1, 2):
                nc.sync.dma_start(columns[:, 8 * d - 8 : 8 * d - 6], gate[d, 0, V // 2 : V].rearrange("(j v) -> v j", v=P))

        nc.scalar.activation(
            w_bf[:, 0:80, :].rearrange("p (c i) j -> p c j i", i=PACK),
            w_raw[:, :, 0:80].rearrange("p j (c i) -> p c j i", i=PACK),
            ACT.Copy,
        )
        nc.gpsimd.tensor_scalar(
            w_bf[:, 80:N, :], w_raw[:, :, 80:N].rearrange("p j n -> p n j"), 1.0, 0.0, ALU.mult, ALU.add
        )
        nc.vector.quantize_mx(w_codes[:].bitcast(FP8X4), w_scales[:], w_bf[:].rearrange("p n j -> p (n j)"))

        picked_words = [
            keep.tile([P, HALF], U32, name="picked_words0", align_bytes=64),
            keep.tile([P, HALF], U32, name="picked_words1", tag="w_then_words", align_bytes=64),
        ]
        for c0, c1 in WORD_GATHERS:
            nc.vector.tensor_copy(
                picked_words[c0 // HALF][:, c0 % HALF : c0 % HALF + c1 - c0],
                word_store[:].bitcast(U32).indirect(entries(offs_sb, c0, c1)),
            )

        accs = []
        for i, (c0, c1) in enumerate(PIECES):
            acc = psum.tile([P, c1 - c0], F32, name="acc%d" % i, tag="bank%d" % i)
            accs.append(acc)
            part = 0 if c0 < SCALE_PARTS[1][0] else 1
            in_part = c0 - SCALE_PARTS[part][0]
            nc.tensor.matmul_mx(
                out=acc[:],
                lhsT=w_codes[:].bitcast(FP8X4),
                lhsT_scale=w_scales[:],
                rhs=picked_words[c0 // HALF][:, c0 % HALF : c0 % HALF + c1 - c0].bitcast(FP8X4),
                rhs_scale=planes[part][:, in_part : in_part + c1 - c0],
                start=True,
                stop=True,
            )

        piece_cols = [slice(c0, c1) for c0, c1 in PIECES]
        for i, cols in enumerate(piece_cols):
            nc.scalar.activation(rect[:, cols], accs[i][:], ACT.Relu, bias=bias[:])
        for cols in piece_cols:
            nc.vector.tensor_tensor(y[:, cols], rect[:, cols], rect[:, cols], ALU.mult)

        blocks = [slice(j * P, (j + 1) * P) for j in range(BLOCKS)]
        front, rear = slice(0, V // 2), slice(V // 2, V)
        for d, cols in ((1, rear), (2, blocks[2]), (2, blocks[3])):
            nc.scalar.activation(terms[:, d, cols], y[:].indirect(entries(pos_sb[d], cols.start, cols.stop)), ACT.Copy)
        turns = [(d, j) for d in (1, 2) for j in (2, 3)]
        forth = [psum.tile([P, P], F32, name="forth%d" % i, tag="bank%d" % i) for i in range(len(turns))]
        for bank, (d, j) in zip(forth, turns):
            nc.tensor.transpose(bank[:], terms[:, d, blocks[j]], ident[:])
        back = {j: psum.tile([P, P], F32, name="back%d" % j, tag="bank%d" % (2 + j)) for j in (2, 3)}
        for i, (d, j) in enumerate(turns):
            column = (d - 1) * 8 + j - 2
            nc.scalar.activation(turned[i][:], forth[i][:], ACT.Copy, scale=columns[:, column : column + 1])
            nc.tensor.matmul(back[j][:], turned[i][:], ident[:], start=(d == 1), stop=(d == 2), is_transpose=True)

        def fetch(d, cols, gates, into):
            nc.vector.tensor_tensor(into, y[:].indirect(entries(pos_sb[d], cols.start, cols.stop)), gates, ALU.mult)

        def finish(j, first, second):
            nc.vector.tensor_tensor(total[:, blocks[j]], first, second, ALU.add)
            nc.sync.dma_start(out[:, blocks[j]], total[:, blocks[j]])

        for d in (1, 2, 0):
            fetch(d, front, gate_front[:, d, :], terms[:, d, front])
        nc.vector.tensor_tensor(partial[:], terms[:, 1, front], terms[:, 2, front], ALU.add)
        own = {2: terms[:, 0, blocks[2]], 3: terms[:, 1, blocks[0]]}
        fetch(0, blocks[2], gate_rear[:, 0:P], own[2])
        finish(0, partial[:, blocks[0]], terms[:, 0, blocks[0]])
        fetch(0, blocks[3], gate_rear[:, P : 2 * P], own[3])
        finish(1, partial[:, blocks[1]], terms[:, 0, blocks[1]])
        for j in (2, 3):
            finish(j, back[j][:], own[j])
